import numpy as np
import ml_dtypes


def mxq(x, axis, fmt="e4m3"):
    dtype, down = {"e4m3": (ml_dtypes.float8_e4m3fn, 7), "e5m2": (ml_dtypes.float8_e5m2, 14)}[fmt]
    v = np.moveaxis(np.asarray(x, np.float32).astype(ml_dtypes.bfloat16).astype(np.float64), axis, -1)
    blocks = v.reshape(v.shape[:-1] + (-1, 32))
    amax = np.abs(blocks).max(-1, keepdims=True)
    byte = np.maximum(np.where(amax > 0, np.frexp(amax)[1] - 1 + 127, 0) - down, 1)
    scale = np.exp2(byte - 127.0)
    codes = (blocks / scale).astype(np.float32).astype(dtype).astype(np.float64)
    return np.moveaxis((codes * scale).reshape(v.shape), -1, axis)


WIDE = False


def mx_kscale(k):
    if not WIDE:
        return np.ones(k)
    levels = np.array([10, -10, 5, -5, 0])
    if k % 512:
        return np.exp2(np.random.permutation(np.resize(levels, k // 32))).repeat(32)
    a = np.empty((k // 512, 16))
    for p in range(k // 512):
        a[p, :8] = np.random.permutation(np.resize(levels, 8))
        for g in range(8):
            far = levels[np.abs(levels - a[p, g]) >= 10]
            a[p, g + 8] = far[np.random.randint(len(far))]
    return np.exp2(a.ravel()).repeat(32)


def f64(x):
    return np.asarray(x).astype(np.float64)


def striped(idx):
    return np.tile(idx.reshape(-1, 16).T, (8, 1)).astype(np.uint16)


def unstriped(offs):
    return offs[:16].T.reshape(-1).astype(np.int64)


def pack_weight(w):
    k, n = w.shape
    w = f64(np.asarray(w, np.float32).astype(ml_dtypes.bfloat16)).reshape(k // 32, 32, n)
    amax = np.abs(w).max(1)
    byte = np.clip(np.where(amax > 0, np.frexp(amax)[1] - 1 + 127 - 7, 1), 1, 254)
    scaled = (w * np.exp2(127.0 - byte)[:, None, :]).reshape(k, n).astype(np.float32)
    words = np.ascontiguousarray(scaled.reshape(k // 512, 128, 4, n).transpose(0, 1, 3, 2)).astype(ml_dtypes.float8_e4m3fn).view(np.uint8)
    return words, np.ascontiguousarray(byte.astype(np.uint8).reshape(k // 512, 16, n))


def unpack_weight(words, scales):
    g, p, n, _ = words.shape
    vals = np.ascontiguousarray(words).view(ml_dtypes.float8_e4m3fn).astype(np.float64) * np.repeat(np.exp2(scales.astype(np.float64) - 127.0), 8, axis=1)[..., None]
    return vals.transpose(0, 1, 3, 2).reshape(g * 512, n)


def gelu(v):
    return 0.5 * v * (1.0 + np.tanh(np.sqrt(2.0 / np.pi) * (v + 0.044715 * v**3)))


K, T, S, N, U = 1024, 2048, 1024, 256, 2048


def setup_inputs():
    n = np.random.standard_normal
    s = mx_kscale(K)[:, None]
    packed_xT = pack_weight(n((K, T)) * s)
    return {
        "x_words": packed_xT[0],
        "x_scales": packed_xT[1],
        "w1": (n((K, N)) / np.sqrt(K) / s).astype(np.float32),
        "res": n((N, U)).astype(np.float32),
        "offs": striped(np.random.permutation(T)[:S]),
        "own": striped(np.random.randint(0, S, U)),
    }


def reference(x_words, x_scales, w1, res, offs, own):
    xq = unpack_weight(x_words, x_scales)[:, unstriped(offs)]
    y = gelu(mxq(f64(w1), 0, "e4m3").T @ xq)
    return f64(res) + y[:, unstriped(own)]

@@ -1,0 +1,132 @@
+from contextlib import ExitStack
+
+import concourse.mybir as mybir
+
+K, T, S, N, U = 1024, 2048, 1024, 256, 2048
+FLOPS = 2 * K * N * S
+
+F32 = mybir.dt.float32
+BF16 = mybir.dt.bfloat16
+I32 = mybir.dt.int32
+U32 = mybir.dt.uint32
+U16 = mybir.dt.uint16
+U8 = mybir.dt.uint8
+FP8X4 = mybir.dt.float8_e4m3fn_x4
+GELU = mybir.ActivationFunctionType.Gelu_apprx_tanh
+ADD = mybir.AluOpType.add
+
+P = 128
+PACK = 4
+K_PASS = P * PACK
+PASSES = K // K_PASS
+BLOCKS = N // P
+LIST_ROWS = 16
+PICK_PIECES = ((0, 512), (512, 768), (768, 1024))
+OUT_PIECES = (((0, 512), (512, 1024), (1024, 1536), (1536, 2048)),
+              ((0, 512), (512, 1024), (1024, 1536), (1536, 1792), (1792, 2048)))
+
+
+def entries(list_tile, lo, hi):
+    return list_tile[:, lo // LIST_ROWS : hi // LIST_ROWS]
+
+
+def tile_picked_unmerge_gelu_p_kernel(tc, x_words, x_scales, w1, res, offs, own, out):
+    nc = tc.nc
+    with ExitStack() as ctx:
+        held = ctx.enter_context(tc.tile_pool(name="held", bufs=1))
+        psum = ctx.enter_context(tc.psum_pool(name="psum", bufs=1))
+
+        offs_sb = held.tile([P, S // LIST_ROWS], U16, name="offs_sb")
+        own_sb = held.tile([P, U // LIST_ROWS], U16, name="own_sb")
+        scale_table = held.tile([P, T], U8, name="scale_table", align_bytes=64)
+        nc.vector.memset(scale_table[:].bitcast(I32), 0)
+        warm_in = held.tile([P, 1], F32, name="warm_in")
+        warm_out = held.tile([P, 1], F32, name="warm_out")
+        nc.gpsimd.memset(warm_in[:], 0.0)
+        nc.scalar.activation(warm_out[:], warm_in[:], GELU)
+
+        def load_w(z, b):
+            raw = held.tile([P, PACK, P], F32, name=f"w_raw{z}{b}")
+            rows = w1[z * K_PASS : (z + 1) * K_PASS, b * P : (b + 1) * P]
+            nc.sync.dma_start(raw[:], rows.rearrange("(p j) c -> p j c", j=PACK))
+            return raw
+
+        def load_words(z):
+            table = held.tile([P, T], I32, name=f"word_table{z}", align_bytes=64)
+            nc.sync.dma_start(table[:], x_words[z].rearrange("p c r -> p (c r)").bitcast(I32))
+            return table
+
+        w_raw = {}
+        nc.sync.dma_start(offs_sb[:], offs)
+        nc.sync.dma_start(own_sb[:], own)
+        for q in range(4):
+            nc.sync.dma_start(scale_table[32 * q : 32 * q + 4 * PASSES, :].bitcast(I32),
+                              x_scales[:, 4 * q : 4 * q + 4, :].bitcast(I32))
+        word_table = [load_words(0)]
+        w_raw[0, 0] = load_w(0, 0)
+        word_table.append(load_words(1))
+        w_raw[1, 0] = load_w(1, 0)
+        w_raw[0, 1] = load_w(0, 1)
+        w_raw[1, 1] = load_w(1, 1)
+        res_sb = {}
+        for b in range(BLOCKS):
+            for h in range(2):
+                t = held.tile([P, U // 2], F32, name=f"res{b}{h}")
+                nc.sync.dma_start(t[:], res[b * P : (b + 1) * P, h * (U // 2) : (h + 1) * (U // 2)])
+                res_sb[b, h] = t
+
+        def cast_w(z, b, tag):
+            grouped = held.tile([P, P * PACK], BF16, name=f"w_bf{z}{b}", tag=tag, align_bytes=64)
+            nc.scalar.copy(grouped[:].rearrange("p (c i j) -> p c j i", i=4, j=PACK),
+                           w_raw[z, b][:].rearrange("p j (c i) -> p c j i", i=4))
+            return grouped
+
+        def quantize_w(z, b, grouped):
+            codes = held.tile([P, P], U32, name=f"w_codes{z}{b}", align_bytes=64)
+            scales = held.tile([P, P], U8, name=f"w_scales{z}{b}", align_bytes=64)
+            nc.vector.quantize_mx(out=codes[:].bitcast(FP8X4), scales=scales[:], in_=grouped[:])
+            return codes, scales
+
+        def gather_words(z, lo, hi, tag):
+            picked = held.tile([P, hi - lo], U32, name=f"picked{z}_{lo}", tag=tag, align_bytes=64)
+            nc.vector.tensor_copy(picked[:], word_table[z][:].bitcast(U32).indirect(entries(offs_sb, lo, hi)))
+            return picked
+
+        picked_scales = held.tile([P, S], U8, name="picked_scales", align_bytes=64)
+        nc.vector.tensor_copy(picked_scales[:], scale_table[:].indirect(offs_sb[:]))
+
+        w_q = {}
+        picked0 = gather_words(0, 0, S, "picked0")
+        w_q[0, 0] = quantize_w(0, 0, cast_w(0, 0, "w_bf00"))
+        picked1 = {}
+        for lo, hi in PICK_PIECES[:-1]:
+            picked1[lo] = gather_words(1, lo, hi, f"picked1_{lo}")
+        w_q[1, 0] = quantize_w(1, 0, cast_w(1, 0, "late"))
+        lo, hi = PICK_PIECES[-1]
+        picked1[lo] = gather_words(1, lo, hi, "late")
+
+        def product(b):
+            y = held.tile([P, S], F32, name=f"y{b}")
+            for lo, hi in PICK_PIECES:
+                acc = psum.tile([P, hi - lo], F32, name=f"acc{b}_{lo}")
+                for z in range(PASSES):
+                    codes, scales = w_q[z, b]
+                    moving = picked0[:, lo:hi] if z == 0 else picked1[lo][:]
+                    nc.tensor.matmul_mx(out=acc[:], lhsT=codes[:].bitcast(FP8X4), lhsT_scale=scales[:],
+                                        rhs=moving.bitcast(FP8X4), rhs_scale=picked_scales[4 * z :, lo:hi],
+                                        start=(z == 0), stop=(z == PASSES - 1))
+                nc.scalar.activation(y[:, lo:hi], acc[:], GELU)
+            return y
+
+        y = [product(0)]
+        for z in range(PASSES):
+            w_q[z, 1] = quantize_w(z, 1, cast_w(z, 1, f"w_bf{z}1"))
+        y.append(product(1))
+
+        for b in range(BLOCKS):
+            for lo, hi in OUT_PIECES[b]:
+                h, at = divmod(lo, U // 2)
+                total = held.tile([P, hi - lo], F32, name=f"total{b}_{lo}")
+                nc.vector.tensor_tensor(total[:], y[b][:].indirect(entries(own_sb, lo, hi)),
+                                        res_sb[b, h][:, at : at + hi - lo], ADD)
+                nc.sync.dma_start(out[b * P : (b + 1) * P, lo:hi], total[:])

@@ -23,7 +23,9 @@ BLOCKS = N // P
 LIST_ROWS = 16
 PICK_PIECES = ((0, 512), (512, 768), (768, 1024))
 OUT_PIECES = (((0, 512), (512, 1024), (1024, 1536), (1536, 2048)),
-              ((0, 512), (512, 1024), (1024, 1536), (1536, 1792), (1792, 2048)))
+              ((0, 512), (512, 1024), (1024, 1536), (1536, 1792), (1792, 1920), (1920, 2048)))
+RES_PIECES = (((0, 512), (512, 2048)), ((0, 2048),))
+MM_PIECES = (((0, 256), (256, 512), (512, 768), (768, 1024)), PICK_PIECES)
 
 
 def entries(list_tile, lo, hi):
@@ -46,7 +48,7 @@ def tile_picked_unmerge_gelu_p_kernel(tc, x_words, x_scales, w1, res, offs, own,
         nc.scalar.activation(warm_out[:], warm_in[:], GELU)
 
         def load_w(z, b):
-            raw = held.tile([P, PACK, P], F32, name=f"w_raw{z}{b}")
+            raw = held.tile([P, PACK, P], F32, name=f"w_raw{z}{b}", tag=f"w_raw{z}{b}", align_bytes=64)
             rows = w1[z * K_PASS : (z + 1) * K_PASS, b * P : (b + 1) * P]
             nc.sync.dma_start(raw[:], rows.rearrange("(p j) c -> p j c", j=PACK))
             return raw
@@ -70,19 +72,19 @@ def tile_picked_unmerge_gelu_p_kernel(tc, x_words, x_scales, w1, res, offs, own,
         w_raw[1, 1] = load_w(1, 1)
         res_sb = {}
         for b in range(BLOCKS):
-            for h in range(2):
-                t = held.tile([P, U // 2], F32, name=f"res{b}{h}")
-                nc.sync.dma_start(t[:], res[b * P : (b + 1) * P, h * (U // 2) : (h + 1) * (U // 2)])
-                res_sb[b, h] = t
+            for lo, hi in RES_PIECES[b]:
+                t = held.tile([P, hi - lo], F32, name=f"res{b}_{lo}")
+                nc.sync.dma_start(t[:], res[b * P : (b + 1) * P, lo:hi])
+                res_sb[b, lo] = t
 
-        def cast_w(z, b, tag):
+        def cast_w(z, b, tag, copy):
             grouped = held.tile([P, P * PACK], BF16, name=f"w_bf{z}{b}", tag=tag, align_bytes=64)
-            nc.scalar.copy(grouped[:].rearrange("p (c i j) -> p c j i", i=4, j=PACK),
+            copy(grouped[:].rearrange("p (c i j) -> p c j i", i=4, j=PACK),
                            w_raw[z, b][:].rearrange("p j (c i) -> p c j i", i=4))
             return grouped
 
         def quantize_w(z, b, grouped):
-            codes = held.tile([P, P], U32, name=f"w_codes{z}{b}", align_bytes=64)
+            codes = held.tile([P, P], U32, name=f"w_codes{z}{b}", tag=f"w_codes{z}{b}", align_bytes=64)
             scales = held.tile([P, P], U8, name=f"w_scales{z}{b}", align_bytes=64)
             nc.vector.quantize_mx(out=codes[:].bitcast(FP8X4), scales=scales[:], in_=grouped[:])
             return codes, scales
@@ -97,21 +99,22 @@ def tile_picked_unmerge_gelu_p_kernel(tc, x_words, x_scales, w1, res, offs, own,
 
         w_q = {}
         picked0 = gather_words(0, 0, S, "picked0")
-        w_q[0, 0] = quantize_w(0, 0, cast_w(0, 0, "w_bf00"))
+        w_q[0, 0] = quantize_w(0, 0, cast_w(0, 0, "w_bf00", nc.scalar.copy))
         picked1 = {}
         for lo, hi in PICK_PIECES[:-1]:
             picked1[lo] = gather_words(1, lo, hi, f"picked1_{lo}")
-        w_q[1, 0] = quantize_w(1, 0, cast_w(1, 0, "late"))
+        w_q[1, 0] = quantize_w(1, 0, cast_w(1, 0, "w_bf10", nc.scalar.copy))
         lo, hi = PICK_PIECES[-1]
-        picked1[lo] = gather_words(1, lo, hi, "late")
+        picked1[lo] = gather_words(1, lo, hi, "w_raw10")
 
         def product(b):
             y = held.tile([P, S], F32, name=f"y{b}")
-            for lo, hi in PICK_PIECES:
+            for lo, hi in MM_PIECES[b]:
+                at = max(start for start, end in PICK_PIECES if start <= lo)
                 acc = psum.tile([P, hi - lo], F32, name=f"acc{b}_{lo}")
                 for z in range(PASSES):
                     codes, scales = w_q[z, b]
-                    moving = picked0[:, lo:hi] if z == 0 else picked1[lo][:]
+                    moving = picked0[:, lo:hi] if z == 0 else picked1[at][:, lo - at : hi - at]
                     nc.tensor.matmul_mx(out=acc[:], lhsT=codes[:].bitcast(FP8X4), lhsT_scale=scales[:],
                                         rhs=moving.bitcast(FP8X4), rhs_scale=picked_scales[4 * z :, lo:hi],
                                         start=(z == 0), stop=(z == PASSES - 1))
@@ -119,14 +122,16 @@ def tile_picked_unmerge_gelu_p_kernel(tc, x_words, x_scales, w1, res, offs, own,
             return y
 
         y = [product(0)]
-        for z in range(PASSES):
-            w_q[z, 1] = quantize_w(z, 1, cast_w(z, 1, f"w_bf{z}1"))
+        grouped01 = cast_w(0, 1, "w_bf01", nc.scalar.copy)
+        grouped11 = cast_w(1, 1, "w_bf11", nc.vector.tensor_copy)
+        w_q[0, 1] = quantize_w(0, 1, grouped01)
+        w_q[1, 1] = quantize_w(1, 1, grouped11)
         y.append(product(1))
 
         for b in range(BLOCKS):
             for lo, hi in OUT_PIECES[b]:
-                h, at = divmod(lo, U // 2)
+                at = max(start for start, end in RES_PIECES[b] if start <= lo)
                 total = held.tile([P, hi - lo], F32, name=f"total{b}_{lo}")
                 nc.vector.tensor_tensor(total[:], y[b][:].indirect(entries(own_sb, lo, hi)),
-                                        res_sb[b, h][:, at : at + hi - lo], ADD)
+                                        res_sb[b, at][:, lo - at : hi - at], ADD)
                 nc.sync.dma_start(out[b * P : (b + 1) * P, lo:hi], total[:])

@@ -25,7 +25,6 @@ PICK_PIECES = ((0, 512), (512, 768), (768, 1024))
 OUT_PIECES = (((0, 512), (512, 1024), (1024, 1536), (1536, 2048)),
               ((0, 512), (512, 1024), (1024, 1536), (1536, 1792), (1792, 1920), (1920, 2048)))
 RES_PIECES = (((0, 512), (512, 2048)), ((0, 2048),))
-MM_PIECES = (((0, 256), (256, 512), (512, 768), (768, 1024)), PICK_PIECES)
 
 
 def entries(list_tile, lo, hi):
@@ -36,97 +35,113 @@ def tile_picked_unmerge_gelu_p_kernel(tc, x_words, x_scales, w1, res, offs, own,
     nc = tc.nc
     with ExitStack() as ctx:
         held = ctx.enter_context(tc.tile_pool(name="held", bufs=1))
+        shared = ctx.enter_context(tc.tile_pool(name="shared", bufs=1))
         psum = ctx.enter_context(tc.psum_pool(name="psum", bufs=1))
 
         offs_sb = held.tile([P, S // LIST_ROWS], U16, name="offs_sb")
         own_sb = held.tile([P, U // LIST_ROWS], U16, name="own_sb")
-        scale_table = held.tile([P, T], U8, name="scale_table", align_bytes=64)
+        KB = 1024
+        scale_table = shared.tile([P, T], U8, name="scale_table", offset=1 * KB)
         nc.vector.memset(scale_table[:].bitcast(I32), 0)
+        planes = held.tile([P, PASSES * S], U8, name="planes", align_bytes=64)
+        nc.vector.memset(planes[:].bitcast(I32), 0)
         warm_in = held.tile([P, 1], F32, name="warm_in")
         warm_out = held.tile([P, 1], F32, name="warm_out")
-        nc.gpsimd.memset(warm_in[:], 0.0)
+        nc.vector.memset(warm_in[:], 0.0)
         nc.scalar.activation(warm_out[:], warm_in[:], GELU)
 
-        def load_w(z, b):
-            raw = held.tile([P, PACK, P], F32, name=f"w_raw{z}{b}", tag=f"w_raw{z}{b}", align_bytes=64)
+        def load_w(z, b, offset):
+            raw = shared.tile([P, PACK, P], F32, name=f"w_raw{z}{b}", offset=offset)
             rows = w1[z * K_PASS : (z + 1) * K_PASS, b * P : (b + 1) * P]
             nc.sync.dma_start(raw[:], rows.rearrange("(p j) c -> p j c", j=PACK))
             return raw
 
-        def load_words(z):
-            table = held.tile([P, T], I32, name=f"word_table{z}", align_bytes=64)
+        def load_words(z, offset):
+            table = shared.tile([P, T], I32, name=f"word_table{z}", offset=offset)
             nc.sync.dma_start(table[:], x_words[z].rearrange("p c r -> p (c r)").bitcast(I32))
             return table
 
+        def load_res(b, lo, hi, offset):
+            t = shared.tile([P, hi - lo], F32, name=f"res{b}_{lo}", offset=offset)
+            nc.sync.dma_start(t[:], res[b * P : (b + 1) * P, lo:hi])
+            return t
+
         w_raw = {}
         nc.sync.dma_start(offs_sb[:], offs)
+        w_raw[0, 0] = load_w(0, 0, 4 * KB)
+        for z in range(PASSES):
+            nc.sync.dma_start(scale_table[4 * z : P : 8, :].bitcast(I32), x_scales[z].bitcast(I32))
+        word_table = [load_words(0, 8 * KB), load_words(1, 20 * KB)]
+        w_raw[1, 0] = load_w(1, 0, 6 * KB)
         nc.sync.dma_start(own_sb[:], own)
-        for q in range(4):
-            nc.sync.dma_start(scale_table[32 * q : 32 * q + 4 * PASSES, :].bitcast(I32),
-                              x_scales[:, 4 * q : 4 * q + 4, :].bitcast(I32))
-        word_table = [load_words(0)]
-        w_raw[0, 0] = load_w(0, 0)
-        word_table.append(load_words(1))
-        w_raw[1, 0] = load_w(1, 0)
-        w_raw[0, 1] = load_w(0, 1)
-        w_raw[1, 1] = load_w(1, 1)
-        res_sb = {}
-        for b in range(BLOCKS):
-            for lo, hi in RES_PIECES[b]:
-                t = held.tile([P, hi - lo], F32, name=f"res{b}_{lo}")
-                nc.sync.dma_start(t[:], res[b * P : (b + 1) * P, lo:hi])
-                res_sb[b, lo] = t
 
-        def cast_w(z, b, tag, copy):
-            grouped = held.tile([P, P * PACK], BF16, name=f"w_bf{z}{b}", tag=tag, align_bytes=64)
+        def cast_w(z, b, copy, offset):
+            grouped = shared.tile([P, P * PACK], BF16, name=f"w_bf{z}{b}", offset=offset, align_bytes=64)
             copy(grouped[:].rearrange("p (c i j) -> p c j i", i=4, j=PACK),
                            w_raw[z, b][:].rearrange("p j (c i) -> p c j i", i=4))
             return grouped
 
-        def quantize_w(z, b, grouped):
-            codes = held.tile([P, P], U32, name=f"w_codes{z}{b}", tag=f"w_codes{z}{b}", align_bytes=64)
+        def quantize_w(z, b, grouped, offset):
+            codes = shared.tile([P, P], U32, name=f"w_codes{z}{b}", offset=offset, align_bytes=64)
             scales = held.tile([P, P], U8, name=f"w_scales{z}{b}", align_bytes=64)
             nc.vector.quantize_mx(out=codes[:].bitcast(FP8X4), scales=scales[:], in_=grouped[:])
             return codes, scales
 
-        def gather_words(z, lo, hi, tag):
-            picked = held.tile([P, hi - lo], U32, name=f"picked{z}_{lo}", tag=tag, align_bytes=64)
+        def gather_words(z, lo, hi, offset):
+            picked = shared.tile([P, hi - lo], U32, name=f"picked{z}_{lo}", offset=offset, align_bytes=64)
             nc.vector.tensor_copy(picked[:], word_table[z][:].bitcast(U32).indirect(entries(offs_sb, lo, hi)))
             return picked
 
         picked_scales = held.tile([P, S], U8, name="picked_scales", align_bytes=64)
         nc.vector.tensor_copy(picked_scales[:], scale_table[:].indirect(offs_sb[:]))
-
+        for q in range(4):
+            queue = nc.scalar if q % 2 else nc.sync
+            queue.dma_start(planes[32 * q : 32 * q + 4, :].bitcast(I32).rearrange("p (z c) -> p z c", z=PASSES),
+                            picked_scales[32 * q : 32 * q + 32 : 4, :].bitcast(I32))
+        w_raw[0, 1] = load_w(0, 1, 0)
+        w_raw[1, 1] = load_w(1, 1, 2 * KB)
         w_q = {}
-        picked0 = gather_words(0, 0, S, "picked0")
-        w_q[0, 0] = quantize_w(0, 0, cast_w(0, 0, "w_bf00", nc.scalar.copy))
-        picked1 = {}
-        for lo, hi in PICK_PIECES[:-1]:
-            picked1[lo] = gather_words(1, lo, hi, f"picked1_{lo}")
-        w_q[1, 0] = quantize_w(1, 0, cast_w(1, 0, "w_bf10", nc.scalar.copy))
-        lo, hi = PICK_PIECES[-1]
-        picked1[lo] = gather_words(1, lo, hi, "w_raw10")
+        w_q[0, 0] = quantize_w(0, 0, cast_w(0, 0, nc.scalar.copy, 40 * KB), 44 * KB)
 
-        def product(b):
+        picked0 = gather_words(0, 0, S, 36 * KB)
+        res_sb = {}
+        res_sb[0, 0] = load_res(0, 0, 512, 8 * KB)
+        res_sb[0, 512] = load_res(0, 512, U, 10 * KB)
+        picked1 = {}
+        picked1[0] = gather_words(1, 0, 512, 32 * KB)
+        w_q[1, 0] = quantize_w(1, 0, cast_w(1, 0, nc.scalar.copy, 41 * KB), 45 * KB)
+        picked1[512] = gather_words(1, 512, 768, 6 * KB)
+        picked1[768] = gather_words(1, 768, 1024, 7 * KB)
+        res_sb[1, 0] = load_res(1, 0, U, 24 * KB)
+        grouped01 = cast_w(0, 1, nc.scalar.copy, 42 * KB)
+        grouped11 = cast_w(1, 1, nc.vector.tensor_copy, 20 * KB)
+        w_q[0, 1] = quantize_w(0, 1, grouped01, 21 * KB)
+        w_q[1, 1] = quantize_w(1, 1, grouped11, 46 * KB)
+
+        def moving(z, lo, hi):
+            if z == 0:
+                return picked0[:, lo:hi]
+            at = max(start for start, end in PICK_PIECES if start <= lo)
+            return picked1[at][:, lo - at : hi - at]
+
+        def product(b, groups, banks):
             y = held.tile([P, S], F32, name=f"y{b}")
-            for lo, hi in MM_PIECES[b]:
-                at = max(start for start, end in PICK_PIECES if start <= lo)
-                acc = psum.tile([P, hi - lo], F32, name=f"acc{b}_{lo}")
+            acc = {}
+            for pieces in groups:
                 for z in range(PASSES):
                     codes, scales = w_q[z, b]
-                    moving = picked0[:, lo:hi] if z == 0 else picked1[at][:, lo - at : hi - at]
-                    nc.tensor.matmul_mx(out=acc[:], lhsT=codes[:].bitcast(FP8X4), lhsT_scale=scales[:],
-                                        rhs=moving.bitcast(FP8X4), rhs_scale=picked_scales[4 * z :, lo:hi],
-                                        start=(z == 0), stop=(z == PASSES - 1))
-                nc.scalar.activation(y[:, lo:hi], acc[:], GELU)
+                    for lo, hi in pieces:
+                        if z == 0:
+                            acc[lo] = psum.tile([P, hi - lo], F32, name=f"acc{b}_{lo}", tag=f"bank{banks[lo]}")
+                        nc.tensor.matmul_mx(out=acc[lo][:], lhsT=codes[:].bitcast(FP8X4), lhsT_scale=scales[:],
+                                            rhs=moving(z, lo, hi).bitcast(FP8X4), rhs_scale=planes[:, z * S + lo : z * S + hi],
+                                            start=(z == 0), stop=(z == PASSES - 1))
+                        if z == PASSES - 1:
+                            nc.scalar.activation(y[:, lo:hi], acc[lo][:], GELU)
             return y
 
-        y = [product(0)]
-        grouped01 = cast_w(0, 1, "w_bf01", nc.scalar.copy)
-        grouped11 = cast_w(1, 1, "w_bf11", nc.vector.tensor_copy)
-        w_q[0, 1] = quantize_w(0, 1, grouped01)
-        w_q[1, 1] = quantize_w(1, 1, grouped11)
-        y.append(product(1))
+        y = [product(0, (((0, 256),), ((256, 512),), ((512, 768),), ((768, 896), (896, 1024))), {0: 0, 256: 1, 512: 2, 768: 3, 896: 4}),
+             product(1, tuple((piece,) for piece in PICK_PIECES), {0: 4, 512: 3, 768: 2})]
 
         for b in range(BLOCKS):
             for lo, hi in OUT_PIECES[b]:

@@ -24,7 +24,7 @@ LIST_ROWS = 16
 PICK_PIECES = ((0, 512), (512, 768), (768, 1024))
 OUT_PIECES = (((0, 512), (512, 1024), (1024, 1536), (1536, 2048)),
               ((0, 512), (512, 1024), (1024, 1536), (1536, 1792), (1792, 1920), (1920, 2048)))
-RES_PIECES = (((0, 512), (512, 2048)), ((0, 2048),))
+RES_PIECES = (((0, 512), (512, 1024), (1024, 2048)), ((0, 2048),))
 
 
 def entries(list_tile, lo, hi):
@@ -68,10 +68,13 @@ def tile_picked_unmerge_gelu_p_kernel(tc, x_words, x_scales, w1, res, offs, own,
 
         w_raw = {}
         nc.sync.dma_start(offs_sb[:], offs)
-        w_raw[0, 0] = load_w(0, 0, 4 * KB)
+        w_raw[0, 0] = shared.tile([P, PACK, P], F32, name="w_raw00", offset=4 * KB)
+        rows00 = w1[0:K_PASS, 0:P].rearrange("(p j) c -> p j c", j=PACK)
+        nc.sync.dma_start(w_raw[0, 0][:, 0:2, :], rows00[:, 0:2, :])
         for z in range(PASSES):
             nc.sync.dma_start(scale_table[4 * z : P : 8, :].bitcast(I32), x_scales[z].bitcast(I32))
         word_table = [load_words(0, 8 * KB), load_words(1, 20 * KB)]
+        nc.sync.dma_start(w_raw[0, 0][:, 2:4, :], rows00[:, 2:4, :])
         w_raw[1, 0] = load_w(1, 0, 6 * KB)
         nc.sync.dma_start(own_sb[:], own)
 
@@ -101,21 +104,25 @@ def tile_picked_unmerge_gelu_p_kernel(tc, x_words, x_scales, w1, res, offs, own,
         w_raw[0, 1] = load_w(0, 1, 0)
         w_raw[1, 1] = load_w(1, 1, 2 * KB)
         w_q = {}
-        w_q[0, 0] = quantize_w(0, 0, cast_w(0, 0, nc.scalar.copy, 40 * KB), 44 * KB)
 
         picked0 = gather_words(0, 0, S, 36 * KB)
+        warm_acc = psum.tile([P, 512], F32, name="warm_acc", tag="bank5")
+        for half in range(2):
+            nc.tensor.matmul_mx(out=warm_acc[:], lhsT=picked0[:, 0:P].bitcast(FP8X4), lhsT_scale=picked_scales[:, 0:P],
+                                rhs=picked0[:, 512 * half : 512 * half + 512].bitcast(FP8X4),
+                                rhs_scale=picked_scales[:, 512 * half : 512 * half + 512], start=True, stop=True)
         res_sb = {}
         res_sb[0, 0] = load_res(0, 0, 512, 8 * KB)
-        res_sb[0, 512] = load_res(0, 512, U, 10 * KB)
+        res_sb[0, 512] = load_res(0, 512, 1024, 10 * KB)
+        res_sb[0, 1024] = load_res(0, 1024, U, 12 * KB)
         picked1 = {}
         picked1[0] = gather_words(1, 0, 512, 32 * KB)
+        w_q[0, 0] = quantize_w(0, 0, cast_w(0, 0, nc.scalar.copy, 40 * KB), 44 * KB)
+        picked1[512] = gather_words(1, 512, 768, 4 * KB)
         w_q[1, 0] = quantize_w(1, 0, cast_w(1, 0, nc.scalar.copy, 41 * KB), 45 * KB)
-        picked1[512] = gather_words(1, 512, 768, 6 * KB)
-        picked1[768] = gather_words(1, 768, 1024, 7 * KB)
+        picked1[768] = gather_words(1, 768, 1024, 6 * KB)
         res_sb[1, 0] = load_res(1, 0, U, 24 * KB)
-        grouped01 = cast_w(0, 1, nc.scalar.copy, 42 * KB)
         grouped11 = cast_w(1, 1, nc.vector.tensor_copy, 20 * KB)
-        w_q[0, 1] = quantize_w(0, 1, grouped01, 21 * KB)
         w_q[1, 1] = quantize_w(1, 1, grouped11, 46 * KB)
 
         def moving(z, lo, hi):
@@ -140,8 +147,9 @@ def tile_picked_unmerge_gelu_p_kernel(tc, x_words, x_scales, w1, res, offs, own,
                             nc.scalar.activation(y[:, lo:hi], acc[lo][:], GELU)
             return y
 
-        y = [product(0, (((0, 256),), ((256, 512),), ((512, 768),), ((768, 896), (896, 1024))), {0: 0, 256: 1, 512: 2, 768: 3, 896: 4}),
-             product(1, tuple((piece,) for piece in PICK_PIECES), {0: 4, 512: 3, 768: 2})]
+        y = [product(0, (((0, 256),), ((256, 512),), ((512, 768),), ((768, 896), (896, 1024))), {0: 0, 256: 1, 512: 2, 768: 3, 896: 4})]
+        w_q[0, 1] = quantize_w(0, 1, cast_w(0, 1, nc.scalar.copy, 45 * KB), 42 * KB)
+        y.append(product(1, (((0, 256), (256, 512), (512, 768), (768, 1024)),), {0: 4, 256: 3, 512: 2, 768: 1}))
 
         for b in range(BLOCKS):
             for lo, hi in OUT_PIECES[b]:

@@ -97,12 +97,12 @@ def tile_picked_unmerge_gelu_p_kernel(tc, x_words, x_scales, w1, res, offs, own,
 
         picked_scales = held.tile([P, S], U8, name="picked_scales", align_bytes=64)
         nc.vector.tensor_copy(picked_scales[:], scale_table[:].indirect(offs_sb[:]))
-        for q in range(4):
-            queue = nc.scalar if q % 2 else nc.sync
-            queue.dma_start(planes[32 * q : 32 * q + 4, :].bitcast(I32).rearrange("p (z c) -> p z c", z=PASSES),
-                            picked_scales[32 * q : 32 * q + 32 : 4, :].bitcast(I32))
-        w_raw[0, 1] = load_w(0, 1, 0)
-        w_raw[1, 1] = load_w(1, 1, 2 * KB)
+        for q in (0, 2, 1, 3):
+            nc.sync.dma_start(planes[32 * q : 32 * q + 4, :].bitcast(I32).rearrange("p (z c) -> p z c", z=PASSES),
+                              picked_scales[32 * q : 32 * q + 32 : 4, :].bitcast(I32))
+        w_raw[1, 1] = load_w(1, 1, 0)
+        res_sb = {}
+        res_sb[0, 0] = load_res(0, 0, 512, 2 * KB)
         w_q = {}
 
         picked0 = gather_words(0, 0, S, 36 * KB)
@@ -111,8 +111,7 @@ def tile_picked_unmerge_gelu_p_kernel(tc, x_words, x_scales, w1, res, offs, own,
             nc.tensor.matmul_mx(out=warm_acc[:], lhsT=picked0[:, 0:P].bitcast(FP8X4), lhsT_scale=picked_scales[:, 0:P],
                                 rhs=picked0[:, 512 * half : 512 * half + 512].bitcast(FP8X4),
                                 rhs_scale=picked_scales[:, 512 * half : 512 * half + 512], start=True, stop=True)
-        res_sb = {}
-        res_sb[0, 0] = load_res(0, 0, 512, 8 * KB)
+        w_raw[0, 1] = load_w(0, 1, 8 * KB)
         res_sb[0, 512] = load_res(0, 512, 1024, 10 * KB)
         res_sb[0, 1024] = load_res(0, 1024, U, 12 * KB)
         picked1 = {}
@@ -131,30 +130,33 @@ def tile_picked_unmerge_gelu_p_kernel(tc, x_words, x_scales, w1, res, offs, own,
             at = max(start for start, end in PICK_PIECES if start <= lo)
             return picked1[at][:, lo - at : hi - at]
 
-        def product(b, groups, banks):
+        def product(b, groups, banks, order):
             y = held.tile([P, S], F32, name=f"y{b}")
             acc = {}
             for pieces in groups:
-                for z in range(PASSES):
+                for z in order:
                     codes, scales = w_q[z, b]
                     for lo, hi in pieces:
-                        if z == 0:
+                        if z == order[0]:
                             acc[lo] = psum.tile([P, hi - lo], F32, name=f"acc{b}_{lo}", tag=f"bank{banks[lo]}")
                         nc.tensor.matmul_mx(out=acc[lo][:], lhsT=codes[:].bitcast(FP8X4), lhsT_scale=scales[:],
                                             rhs=moving(z, lo, hi).bitcast(FP8X4), rhs_scale=planes[:, z * S + lo : z * S + hi],
-                                            start=(z == 0), stop=(z == PASSES - 1))
-                        if z == PASSES - 1:
+                                            start=(z == order[0]), stop=(z == order[-1]))
+                        if z == order[-1]:
                             nc.scalar.activation(y[:, lo:hi], acc[lo][:], GELU)
             return y
 
-        y = [product(0, (((0, 256),), ((256, 512),), ((512, 768),), ((768, 896), (896, 1024))), {0: 0, 256: 1, 512: 2, 768: 3, 896: 4})]
+        y = [product(0, (((0, 256),), ((256, 512),), ((512, 768),), ((768, 896), (896, 1024))), {0: 0, 256: 1, 512: 2, 768: 3, 896: 4}, (0, 1))]
         w_q[0, 1] = quantize_w(0, 1, cast_w(0, 1, nc.scalar.copy, 45 * KB), 42 * KB)
-        y.append(product(1, (((0, 256), (256, 512), (512, 768), (768, 1024)),), {0: 4, 256: 3, 512: 2, 768: 1}))
+        y.append(product(1, (((0, 256), (256, 512), (512, 768), (768, 1024)),), {0: 4, 256: 3, 512: 2, 768: 1}, (1, 0)))
 
         for b in range(BLOCKS):
             for lo, hi in OUT_PIECES[b]:
                 at = max(start for start, end in RES_PIECES[b] if start <= lo)
-                total = held.tile([P, hi - lo], F32, name=f"total{b}_{lo}")
+                if (b, lo) == (0, 512):
+                    total = shared.tile([P, hi - lo], F32, name=f"total{b}_{lo}", offset=8 * KB)
+                else:
+                    total = held.tile([P, hi - lo], F32, name=f"total{b}_{lo}")
                 nc.vector.tensor_tensor(total[:], y[b][:].indirect(entries(own_sb, lo, hi)),
                                         res_sb[b, at][:, lo - at : hi - at], ADD)
                 nc.sync.dma_start(out[b * P : (b + 1) * P, lo:hi], total[:])

@@ -106,11 +106,6 @@ def tile_picked_unmerge_gelu_p_kernel(tc, x_words, x_scales, w1, res, offs, own,
         w_q = {}
 
         picked0 = gather_words(0, 0, S, 36 * KB)
-        warm_acc = psum.tile([P, 512], F32, name="warm_acc", tag="bank5")
-        for half in range(2):
-            nc.tensor.matmul_mx(out=warm_acc[:], lhsT=picked0[:, 0:P].bitcast(FP8X4), lhsT_scale=picked_scales[:, 0:P],
-                                rhs=picked0[:, 512 * half : 512 * half + 512].bitcast(FP8X4),
-                                rhs_scale=picked_scales[:, 512 * half : 512 * half + 512], start=True, stop=True)
         w_raw[0, 1] = load_w(0, 1, 8 * KB)
         res_sb[0, 512] = load_res(0, 512, 1024, 10 * KB)
         res_sb[0, 1024] = load_res(0, 1024, U, 12 * KB)

@@ -13,6 +13,7 @@ U16 = mybir.dt.uint16
 U8 = mybir.dt.uint8
 FP8X4 = mybir.dt.float8_e4m3fn_x4
 GELU = mybir.ActivationFunctionType.Gelu_apprx_tanh
+COPY = mybir.ActivationFunctionType.Copy
 ADD = mybir.AluOpType.add
 
 P = 128
@@ -21,10 +22,10 @@ K_PASS = P * PACK
 PASSES = K // K_PASS
 BLOCKS = N // P
 LIST_ROWS = 16
-PICK_PIECES = ((0, 512), (512, 768), (768, 1024))
-OUT_PIECES = (((0, 512), (512, 1024), (1024, 1536), (1536, 2048)),
-              ((0, 512), (512, 1024), (1024, 1536), (1536, 1792), (1792, 1920), (1920, 2048)))
-RES_PIECES = (((0, 512), (512, 1024), (1024, 2048)), ((0, 2048),))
+SCALE_ROWS = 16
+FIRST_SCALE_ROW = P - PASSES * SCALE_ROWS
+PRODUCT_PIECES = ((0, 256), (256, 512), (512, 768), (768, 1024))
+KB = 1024
 
 
 def entries(list_tile, lo, hi):
@@ -40,9 +41,8 @@ def tile_picked_unmerge_gelu_p_kernel(tc, x_words, x_scales, w1, res, offs, own,
 
         offs_sb = held.tile([P, S // LIST_ROWS], U16, name="offs_sb")
         own_sb = held.tile([P, U // LIST_ROWS], U16, name="own_sb")
-        KB = 1024
-        scale_table = shared.tile([P, T], U8, name="scale_table", offset=1 * KB)
-        nc.vector.memset(scale_table[:].bitcast(I32), 0)
+        scale_table = shared.tile([P, T], U8, name="scale_table", offset=24 * KB)
+        nc.vector.memset(scale_table[0:FIRST_SCALE_ROW, :].bitcast(I32), 0)
         planes = held.tile([P, PASSES * S], U8, name="planes", align_bytes=64)
         nc.vector.memset(planes[:].bitcast(I32), 0)
         warm_in = held.tile([P, 1], F32, name="warm_in")
@@ -50,108 +50,123 @@ def tile_picked_unmerge_gelu_p_kernel(tc, x_words, x_scales, w1, res, offs, own,
         nc.vector.memset(warm_in[:], 0.0)
         nc.scalar.activation(warm_out[:], warm_in[:], GELU)
 
-        def load_w(z, b, offset):
-            raw = shared.tile([P, PACK, P], F32, name=f"w_raw{z}{b}", offset=offset)
-            rows = w1[z * K_PASS : (z + 1) * K_PASS, b * P : (b + 1) * P]
-            nc.sync.dma_start(raw[:], rows.rearrange("(p j) c -> p j c", j=PACK))
-            return raw
-
-        def load_words(z, offset):
-            table = shared.tile([P, T], I32, name=f"word_table{z}", offset=offset)
-            nc.sync.dma_start(table[:], x_words[z].rearrange("p c r -> p (c r)").bitcast(I32))
-            return table
-
-        def load_res(b, lo, hi, offset):
-            t = shared.tile([P, hi - lo], F32, name=f"res{b}_{lo}", offset=offset)
-            nc.sync.dma_start(t[:], res[b * P : (b + 1) * P, lo:hi])
-            return t
-
-        w_raw = {}
         nc.sync.dma_start(offs_sb[:], offs)
-        w_raw[0, 0] = shared.tile([P, PACK, P], F32, name="w_raw00", offset=4 * KB)
-        rows00 = w1[0:K_PASS, 0:P].rearrange("(p j) c -> p j c", j=PACK)
-        nc.sync.dma_start(w_raw[0, 0][:, 0:2, :], rows00[:, 0:2, :])
+        nc.sync.dma_start(scale_table[FIRST_SCALE_ROW:P, :].bitcast(I32), x_scales.rearrange("z r c -> r z c").bitcast(I32))
+        word_table = []
+        w_raw = []
+
+        def load_w(z, offset):
+            raw = shared.tile([P, PACK, N], F32, name=f"w_raw{z}", offset=offset)
+            nc.sync.dma_start(raw[:], w1[z * K_PASS : (z + 1) * K_PASS, :].rearrange("(p j) c -> p j c", j=PACK))
+            w_raw.append(raw)
+
         for z in range(PASSES):
-            nc.sync.dma_start(scale_table[4 * z : P : 8, :].bitcast(I32), x_scales[z].bitcast(I32))
-        word_table = [load_words(0, 8 * KB), load_words(1, 20 * KB)]
-        nc.sync.dma_start(w_raw[0, 0][:, 2:4, :], rows00[:, 2:4, :])
-        w_raw[1, 0] = load_w(1, 0, 6 * KB)
+            table = shared.tile([P, T], I32, name=f"word_table{z}", offset=(8 + 8 * z) * KB)
+            nc.sync.dma_start(table[:], x_words[z].rearrange("p c r -> p (c r)").bitcast(I32))
+            word_table.append(table)
+            if z == 0:
+                load_w(0, 0)
         nc.sync.dma_start(own_sb[:], own)
-
-        def cast_w(z, b, copy, offset):
-            grouped = shared.tile([P, P * PACK], BF16, name=f"w_bf{z}{b}", offset=offset, align_bytes=64)
-            copy(grouped[:].rearrange("p (c i j) -> p c j i", i=4, j=PACK),
-                           w_raw[z, b][:].rearrange("p j (c i) -> p c j i", i=4))
-            return grouped
-
-        def quantize_w(z, b, grouped, offset):
-            codes = shared.tile([P, P], U32, name=f"w_codes{z}{b}", offset=offset, align_bytes=64)
-            scales = held.tile([P, P], U8, name=f"w_scales{z}{b}", align_bytes=64)
-            nc.vector.quantize_mx(out=codes[:].bitcast(FP8X4), scales=scales[:], in_=grouped[:])
-            return codes, scales
-
-        def gather_words(z, lo, hi, offset):
-            picked = shared.tile([P, hi - lo], U32, name=f"picked{z}_{lo}", offset=offset, align_bytes=64)
-            nc.vector.tensor_copy(picked[:], word_table[z][:].bitcast(U32).indirect(entries(offs_sb, lo, hi)))
-            return picked
 
         picked_scales = held.tile([P, S], U8, name="picked_scales", align_bytes=64)
         nc.vector.tensor_copy(picked_scales[:], scale_table[:].indirect(offs_sb[:]))
         for q in (0, 2, 1, 3):
+            first = FIRST_SCALE_ROW + 8 * q
             nc.sync.dma_start(planes[32 * q : 32 * q + 4, :].bitcast(I32).rearrange("p (z c) -> p z c", z=PASSES),
-                              picked_scales[32 * q : 32 * q + 32 : 4, :].bitcast(I32))
-        w_raw[1, 1] = load_w(1, 1, 0)
+                              picked_scales[first : first + 8, :].bitcast(I32))
+        load_w(1, 24 * KB)
+
+        picked = {}
+
+        def gather_words(z, lo, hi, offset):
+            picked[z, lo] = shared.tile([P, hi - lo], U32, name=f"picked{z}_{lo}", offset=offset, align_bytes=64)
+            nc.vector.tensor_copy(picked[z, lo][:], word_table[z][:].bitcast(U32).indirect(entries(offs_sb, lo, hi)))
+
+        def picked_cols(z, lo, hi):
+            at = max(start for zz, start in picked if zz == z and start <= lo)
+            return picked[z, at][:, lo - at : hi - at]
+
+        gather_words(0, 0, S, 32 * KB)
         res_sb = {}
-        res_sb[0, 0] = load_res(0, 0, 512, 2 * KB)
+
+        def load_res(b, lo, hi, offset):
+            res_sb[b, lo] = shared.tile([P, hi - lo], F32, name=f"res{b}_{lo}", offset=offset)
+            nc.sync.dma_start(res_sb[b, lo][:], res[b * P : (b + 1) * P, lo:hi])
+
+        load_res(0, 0, 1024, 8 * KB)
+        load_res(0, 1024, 2048, 12 * KB)
+
+        def res_cols(b, lo, hi):
+            at = max(start for block, start in res_sb if block == b and start <= lo)
+            return res_sb[b, at][:, lo - at : hi - at]
+
+        def cast_w(z, b, copy, offset):
+            grouped = shared.tile([P, P * PACK], BF16, name=f"w_bf{z}{b}", offset=offset, align_bytes=64)
+            copy(grouped[:].rearrange("p (c i j) -> p c j i", i=4, j=PACK),
+                 w_raw[z][:, :, b * P : (b + 1) * P].rearrange("p j (c i) -> p c j i", i=4))
+            return grouped
+
+        def quantize_w(z, b, grouped):
+            codes = held.tile([P, P], U32, name=f"w_codes{z}{b}", align_bytes=64)
+            scales = held.tile([P, P], U8, name=f"w_scales{z}{b}", align_bytes=64)
+            nc.vector.quantize_mx(out=codes[:].bitcast(FP8X4), scales=scales[:], in_=grouped[:])
+            return codes, scales
+
         w_q = {}
-
-        picked0 = gather_words(0, 0, S, 36 * KB)
-        w_raw[0, 1] = load_w(0, 1, 8 * KB)
-        res_sb[0, 512] = load_res(0, 512, 1024, 10 * KB)
-        res_sb[0, 1024] = load_res(0, 1024, U, 12 * KB)
-        picked1 = {}
-        picked1[0] = gather_words(1, 0, 512, 32 * KB)
-        w_q[0, 0] = quantize_w(0, 0, cast_w(0, 0, nc.scalar.copy, 40 * KB), 44 * KB)
-        picked1[512] = gather_words(1, 512, 768, 4 * KB)
-        w_q[1, 0] = quantize_w(1, 0, cast_w(1, 0, nc.scalar.copy, 41 * KB), 45 * KB)
-        picked1[768] = gather_words(1, 768, 1024, 6 * KB)
-        res_sb[1, 0] = load_res(1, 0, U, 24 * KB)
-        grouped11 = cast_w(1, 1, nc.vector.tensor_copy, 20 * KB)
-        w_q[1, 1] = quantize_w(1, 1, grouped11, 46 * KB)
-
-        def moving(z, lo, hi):
-            if z == 0:
-                return picked0[:, lo:hi]
-            at = max(start for start, end in PICK_PIECES if start <= lo)
-            return picked1[at][:, lo - at : hi - at]
-
-        def product(b, groups, banks, order):
-            y = held.tile([P, S], F32, name=f"y{b}")
-            acc = {}
-            for pieces in groups:
-                for z in order:
-                    codes, scales = w_q[z, b]
-                    for lo, hi in pieces:
-                        if z == order[0]:
-                            acc[lo] = psum.tile([P, hi - lo], F32, name=f"acc{b}_{lo}", tag=f"bank{banks[lo]}")
-                        nc.tensor.matmul_mx(out=acc[lo][:], lhsT=codes[:].bitcast(FP8X4), lhsT_scale=scales[:],
-                                            rhs=moving(z, lo, hi).bitcast(FP8X4), rhs_scale=planes[:, z * S + lo : z * S + hi],
-                                            start=(z == order[0]), stop=(z == order[-1]))
-                        if z == order[-1]:
-                            nc.scalar.activation(y[:, lo:hi], acc[lo][:], GELU)
-            return y
-
-        y = [product(0, (((0, 256),), ((256, 512),), ((512, 768),), ((768, 896), (896, 1024))), {0: 0, 256: 1, 512: 2, 768: 3, 896: 4}, (0, 1))]
-        w_q[0, 1] = quantize_w(0, 1, cast_w(0, 1, nc.scalar.copy, 45 * KB), 42 * KB)
-        y.append(product(1, (((0, 256), (256, 512), (512, 768), (768, 1024)),), {0: 4, 256: 3, 512: 2, 768: 1}, (1, 0)))
-
         for b in range(BLOCKS):
-            for lo, hi in OUT_PIECES[b]:
-                at = max(start for start, end in RES_PIECES[b] if start <= lo)
-                if (b, lo) == (0, 512):
-                    total = shared.tile([P, hi - lo], F32, name=f"total{b}_{lo}", offset=8 * KB)
-                else:
-                    total = held.tile([P, hi - lo], F32, name=f"total{b}_{lo}")
-                nc.vector.tensor_tensor(total[:], y[b][:].indirect(entries(own_sb, lo, hi)),
-                                        res_sb[b, at][:, lo - at : hi - at], ADD)
-                nc.sync.dma_start(out[b * P : (b + 1) * P, lo:hi], total[:])
+            w_q[0, b] = quantize_w(0, b, cast_w(0, b, nc.scalar.copy, (40 + b) * KB))
+        load_res(1, 0, U, 0)
+        gather_words(1, 0, S, 36 * KB)
+        w_q[1, 0] = quantize_w(1, 0, cast_w(1, 0, nc.scalar.copy, 42 * KB))
+        w_q[1, 1] = quantize_w(1, 1, cast_w(1, 1, nc.vector.tensor_copy, 42 * KB))
+
+        y = [held.tile([P, S], F32, name=f"y{b}") for b in range(BLOCKS)]
+        acc = {}
+
+        def product(b, z, lo, hi):
+            if z == 0:
+                acc[b, lo] = psum.tile([P, hi - lo], F32, name=f"acc{b}_{lo}")
+            codes, scales = w_q[z, b]
+            nc.tensor.matmul_mx(out=acc[b, lo][:], lhsT=codes[:].bitcast(FP8X4), lhsT_scale=scales[:],
+                                rhs=picked_cols(z, lo, hi).bitcast(FP8X4), rhs_scale=planes[:, z * S + lo : z * S + hi],
+                                start=(z == 0), stop=(z == PASSES - 1))
+            if z == PASSES - 1:
+                nc.scalar.activation(y[b][:, lo:hi], acc[b, lo][:], GELU)
+
+        for z in range(PASSES):
+            for b in range(BLOCKS):
+                for lo, hi in PRODUCT_PIECES:
+                    product(b, z, lo, hi)
+
+        def finish(b, lo, hi, looked_up, offset):
+            total = shared.tile([P, hi - lo], F32, name=f"total{b}_{lo}", offset=offset)
+            nc.vector.tensor_tensor(total[:], looked_up, res_cols(b, lo, hi), ADD)
+            nc.sync.dma_start(out[b * P : (b + 1) * P, lo:hi], total[:])
+
+        def on_vector(b, lo, hi, offset):
+            finish(b, lo, hi, y[b][:].indirect(entries(own_sb, lo, hi)), offset)
+
+        fetched = {}
+
+        def fetch(b, lo, hi):
+            fetched[b, lo] = shared.tile([P, hi - lo], F32, name=f"fetched{b}_{lo}", offset=(40 + 8 * b) * KB + 4 * lo)
+            nc.scalar.activation(fetched[b, lo][:], y[b][:].indirect(entries(own_sb, lo, hi)), COPY)
+
+        def add(b, lo, hi):
+            finish(b, lo, hi, fetched[b, lo][:], (56 + 8 * b) * KB + 4 * lo)
+
+        scalar_pieces = ((0, 512), (512, 1024), (1024, 1536), (1536, 1920), (1920, 2048))
+        fetch(0, 1792, 2048)
+        for lo, hi in scalar_pieces:
+            fetch(1, lo, hi)
+        on_vector(0, 0, 512, 56 * KB)
+        on_vector(0, 512, 1024, 58 * KB)
+        on_vector(0, 1024, 1280, 60 * KB)
+        add(0, 1792, 2048)
+        add(1, 0, 512)
+        on_vector(0, 1280, 1536, 48 * KB)
+        add(1, 512, 1024)
+        on_vector(0, 1536, 1792, 49 * KB)
+        add(1, 1024, 1536)
+        add(1, 1536, 1920)
+        add(1, 1920, 2048)

@@ -161,12 +161,8 @@ def tile_picked_unmerge_gelu_p_kernel(tc, x_words, x_scales, w1, res, offs, own,
             fetch(1, lo, hi)
         on_vector(0, 0, 512, 56 * KB)
         on_vector(0, 512, 1024, 58 * KB)
-        on_vector(0, 1024, 1280, 60 * KB)
+        on_vector(0, 1024, 1408, 60 * KB)
+        on_vector(0, 1408, 1792, 60 * KB + 4 * 384)
         add(0, 1792, 2048)
-        add(1, 0, 512)
-        on_vector(0, 1280, 1536, 48 * KB)
-        add(1, 512, 1024)
-        on_vector(0, 1536, 1792, 49 * KB)
-        add(1, 1024, 1536)
-        add(1, 1536, 1920)
-        add(1, 1920, 2048)
+        for lo, hi in scalar_pieces:
+            add(1, lo, hi)

@@ -43,15 +43,16 @@ def tile_picked_unmerge_gelu_p_kernel(tc, x_words, x_scales, w1, res, offs, own,
         own_sb = held.tile([P, U // LIST_ROWS], U16, name="own_sb")
         scale_table = shared.tile([P, T], U8, name="scale_table", offset=24 * KB)
         nc.vector.memset(scale_table[0:FIRST_SCALE_ROW, :].bitcast(I32), 0)
-        planes = held.tile([P, PASSES * S], U8, name="planes", align_bytes=64)
-        nc.vector.memset(planes[:].bitcast(I32), 0)
+        planes = [held.tile([P, S], U8, name=f"plane{z}", align_bytes=64) for z in range(PASSES)]
+        for plane in planes:
+            nc.vector.memset(plane[:].bitcast(I32), 0)
         warm_in = held.tile([P, 1], F32, name="warm_in")
         warm_out = held.tile([P, 1], F32, name="warm_out")
         nc.vector.memset(warm_in[:], 0.0)
         nc.scalar.activation(warm_out[:], warm_in[:], GELU)
 
         nc.sync.dma_start(offs_sb[:], offs)
-        nc.sync.dma_start(scale_table[FIRST_SCALE_ROW:P, :].bitcast(I32), x_scales.rearrange("z r c -> r z c").bitcast(I32))
+        nc.sync.dma_start(scale_table[FIRST_SCALE_ROW:P, :].bitcast(I32), x_scales.rearrange("z r c -> (z r) c").bitcast(I32))
         word_table = []
         w_raw = []
 
@@ -70,11 +71,15 @@ def tile_picked_unmerge_gelu_p_kernel(tc, x_words, x_scales, w1, res, offs, own,
 
         picked_scales = held.tile([P, S], U8, name="picked_scales", align_bytes=64)
         nc.vector.tensor_copy(picked_scales[:], scale_table[:].indirect(offs_sb[:]))
-        for q in (0, 2, 1, 3):
-            first = FIRST_SCALE_ROW + 8 * q
-            nc.sync.dma_start(planes[32 * q : 32 * q + 4, :].bitcast(I32).rearrange("p (z c) -> p z c", z=PASSES),
-                              picked_scales[first : first + 8, :].bitcast(I32))
+
+        def move_scales(z):
+            for q in (0, 2, 1, 3):
+                first = FIRST_SCALE_ROW + SCALE_ROWS * z + 4 * q
+                nc.sync.dma_start(planes[z][32 * q : 32 * q + 4, :].bitcast(I32), picked_scales[first : first + 4, :].bitcast(I32))
+
+        move_scales(0)
         load_w(1, 24 * KB)
+        move_scales(1)
 
         picked = {}
 
@@ -128,41 +133,53 @@ def tile_picked_unmerge_gelu_p_kernel(tc, x_words, x_scales, w1, res, offs, own,
                 acc[b, lo] = psum.tile([P, hi - lo], F32, name=f"acc{b}_{lo}")
             codes, scales = w_q[z, b]
             nc.tensor.matmul_mx(out=acc[b, lo][:], lhsT=codes[:].bitcast(FP8X4), lhsT_scale=scales[:],
-                                rhs=picked_cols(z, lo, hi).bitcast(FP8X4), rhs_scale=planes[:, z * S + lo : z * S + hi],
+                                rhs=picked_cols(z, lo, hi).bitcast(FP8X4), rhs_scale=planes[z][:, lo:hi],
                                 start=(z == 0), stop=(z == PASSES - 1))
             if z == PASSES - 1:
                 nc.scalar.activation(y[b][:, lo:hi], acc[b, lo][:], GELU)
 
-        for z in range(PASSES):
-            for b in range(BLOCKS):
-                for lo, hi in PRODUCT_PIECES:
-                    product(b, z, lo, hi)
+        for b, z in ((0, 0), (1, 0), (0, 1)):
+            for lo, hi in PRODUCT_PIECES:
+                product(b, z, lo, hi)
 
-        def finish(b, lo, hi, looked_up, offset):
-            total = shared.tile([P, hi - lo], F32, name=f"total{b}_{lo}", offset=offset)
-            nc.vector.tensor_tensor(total[:], looked_up, res_cols(b, lo, hi), ADD)
-            nc.sync.dma_start(out[b * P : (b + 1) * P, lo:hi], total[:])
-
-        def on_vector(b, lo, hi, offset):
-            finish(b, lo, hi, y[b][:].indirect(entries(own_sb, lo, hi)), offset)
-
+        total = [held.tile([P, U], F32, name=f"total{b}") for b in range(BLOCKS)]
         fetched = {}
 
+        def on_vector(b, lo, hi):
+            nc.vector.tensor_tensor(total[b][:, lo:hi], y[b][:].indirect(entries(own_sb, lo, hi)), res_cols(b, lo, hi), ADD)
+
         def fetch(b, lo, hi):
-            fetched[b, lo] = shared.tile([P, hi - lo], F32, name=f"fetched{b}_{lo}", offset=(40 + 8 * b) * KB + 4 * lo)
+            fetched[b, lo] = held.tile([P, hi - lo], F32, name=f"fetched{b}_{lo}")
             nc.scalar.activation(fetched[b, lo][:], y[b][:].indirect(entries(own_sb, lo, hi)), COPY)
 
         def add(b, lo, hi):
-            finish(b, lo, hi, fetched[b, lo][:], (56 + 8 * b) * KB + 4 * lo)
+            nc.vector.tensor_tensor(total[b][:, lo:hi], fetched[b, lo][:], res_cols(b, lo, hi), ADD)
 
-        scalar_pieces = ((0, 512), (512, 1024), (1024, 1536), (1536, 1920), (1920, 2048))
-        fetch(0, 1792, 2048)
-        for lo, hi in scalar_pieces:
+        def store(b, lo, hi):
+            nc.sync.dma_start(out[b * P : (b + 1) * P, lo:hi], total[b][:, lo:hi])
+
+        for lo, hi in PRODUCT_PIECES:
+            product(1, 1, lo, hi)
+        fetch(0, 1536, 2048)
+        for lo, hi in ((0, 512), (512, 1024), (1280, 1664), (1664, 1920), (1920, 2048)):
             fetch(1, lo, hi)
-        on_vector(0, 0, 512, 56 * KB)
-        on_vector(0, 512, 1024, 58 * KB)
-        on_vector(0, 1024, 1408, 60 * KB)
-        on_vector(0, 1408, 1792, 60 * KB + 4 * 384)
-        add(0, 1792, 2048)
-        for lo, hi in scalar_pieces:
-            add(1, lo, hi)
+        on_vector(0, 0, 512)
+        store(0, 0, 512)
+        on_vector(0, 512, 1024)
+        store(0, 512, 1024)
+        on_vector(0, 1024, 1536)
+        store(0, 1024, 1536)
+        add(0, 1536, 2048)
+        store(0, 1536, 2048)
+        add(1, 0, 512)
+        store(1, 0, 512)
+        add(1, 512, 1024)
+        store(1, 512, 1024)
+        on_vector(1, 1024, 1280)
+        store(1, 1024, 1280)
+        add(1, 1280, 1664)
+        store(1, 1280, 1664)
+        add(1, 1664, 1920)
+        store(1, 1664, 1920)
+        add(1, 1920, 2048)
+        store(1, 1920, 2048)

@@ -24,7 +24,7 @@ BLOCKS = N // P
 LIST_ROWS = 16
 SCALE_ROWS = 16
 FIRST_SCALE_ROW = P - PASSES * SCALE_ROWS
-PRODUCT_PIECES = ((0, 256), (256, 512), (512, 768), (768, 1024))
+PRODUCT_PIECES = ((0, 256), (256, 768), (768, 896), (896, 1024))
 KB = 1024
 
 
@@ -41,7 +41,7 @@ def tile_picked_unmerge_gelu_p_kernel(tc, x_words, x_scales, w1, res, offs, own,
 
         offs_sb = held.tile([P, S // LIST_ROWS], U16, name="offs_sb")
         own_sb = held.tile([P, U // LIST_ROWS], U16, name="own_sb")
-        scale_table = shared.tile([P, T], U8, name="scale_table", offset=24 * KB)
+        scale_table = shared.tile([P, T], U8, name="scale_table", offset=27 * KB)
         nc.vector.memset(scale_table[0:FIRST_SCALE_ROW, :].bitcast(I32), 0)
         planes = [held.tile([P, S], U8, name=f"plane{z}", align_bytes=64) for z in range(PASSES)]
         for plane in planes:
@@ -72,6 +72,12 @@ def tile_picked_unmerge_gelu_p_kernel(tc, x_words, x_scales, w1, res, offs, own,
         picked_scales = held.tile([P, S], U8, name="picked_scales", align_bytes=64)
         nc.vector.tensor_copy(picked_scales[:], scale_table[:].indirect(offs_sb[:]))
 
+        res_sb = {}
+
+        def load_res(b, lo, hi, offset):
+            res_sb[b, lo] = shared.tile([P, hi - lo], F32, name=f"res{b}_{lo}", offset=offset)
+            nc.sync.dma_start(res_sb[b, lo][:], res[b * P : (b + 1) * P, lo:hi])
+
         def move_scales(z):
             for q in (0, 2, 1, 3):
                 first = FIRST_SCALE_ROW + SCALE_ROWS * z + 4 * q
@@ -79,6 +85,7 @@ def tile_picked_unmerge_gelu_p_kernel(tc, x_words, x_scales, w1, res, offs, own,
 
         move_scales(0)
         load_w(1, 24 * KB)
+        load_res(0, 0, 512, 28 * KB)
         move_scales(1)
 
         picked = {}
@@ -92,14 +99,7 @@ def tile_picked_unmerge_gelu_p_kernel(tc, x_words, x_scales, w1, res, offs, own,
             return picked[z, at][:, lo - at : hi - at]
 
         gather_words(0, 0, S, 32 * KB)
-        res_sb = {}
-
-        def load_res(b, lo, hi, offset):
-            res_sb[b, lo] = shared.tile([P, hi - lo], F32, name=f"res{b}_{lo}", offset=offset)
-            nc.sync.dma_start(res_sb[b, lo][:], res[b * P : (b + 1) * P, lo:hi])
-
-        load_res(0, 0, 1024, 8 * KB)
-        load_res(0, 1024, 2048, 12 * KB)
+        load_res(0, 512, U, 8 * KB)
 
         def res_cols(b, lo, hi):
             at = max(start for block, start in res_sb if block == b and start <= lo)
@@ -121,9 +121,11 @@ def tile_picked_unmerge_gelu_p_kernel(tc, x_words, x_scales, w1, res, offs, own,
         for b in range(BLOCKS):
             w_q[0, b] = quantize_w(0, b, cast_w(0, b, nc.scalar.copy, (40 + b) * KB))
         load_res(1, 0, U, 0)
-        gather_words(1, 0, S, 36 * KB)
+        gather_words(1, 0, 896, 36 * KB)
         w_q[1, 0] = quantize_w(1, 0, cast_w(1, 0, nc.scalar.copy, 42 * KB))
-        w_q[1, 1] = quantize_w(1, 1, cast_w(1, 1, nc.vector.tensor_copy, 42 * KB))
+        grouped11 = cast_w(1, 1, nc.scalar.copy, 43 * KB)
+        gather_words(1, 896, S, 24 * KB)
+        w_q[1, 1] = quantize_w(1, 1, grouped11)
 
         y = [held.tile([P, S], F32, name=f"y{b}") for b in range(BLOCKS)]
         acc = {}

@@ -24,7 +24,7 @@ BLOCKS = N // P
 LIST_ROWS = 16
 SCALE_ROWS = 16
 FIRST_SCALE_ROW = P - PASSES * SCALE_ROWS
-PRODUCT_PIECES = ((0, 256), (256, 768), (768, 896), (896, 1024))
+PRODUCT_PIECES = (((0, 256), (256, 512), (512, 768), (768, 896), (896, 1024)), ((0, 512), (512, 768), (768, 896), (896, 1024)))
 KB = 1024
 
 
@@ -43,16 +43,15 @@ def tile_picked_unmerge_gelu_p_kernel(tc, x_words, x_scales, w1, res, offs, own,
         own_sb = held.tile([P, U // LIST_ROWS], U16, name="own_sb")
         scale_table = shared.tile([P, T], U8, name="scale_table", offset=27 * KB)
         nc.vector.memset(scale_table[0:FIRST_SCALE_ROW, :].bitcast(I32), 0)
-        planes = [held.tile([P, S], U8, name=f"plane{z}", align_bytes=64) for z in range(PASSES)]
-        for plane in planes:
-            nc.vector.memset(plane[:].bitcast(I32), 0)
+        planes = held.tile([P, PASSES * S], U8, name="planes", align_bytes=64)
+        nc.vector.memset(planes[:].bitcast(I32), 0)
         warm_in = held.tile([P, 1], F32, name="warm_in")
         warm_out = held.tile([P, 1], F32, name="warm_out")
         nc.vector.memset(warm_in[:], 0.0)
         nc.scalar.activation(warm_out[:], warm_in[:], GELU)
 
         nc.sync.dma_start(offs_sb[:], offs)
-        nc.sync.dma_start(scale_table[FIRST_SCALE_ROW:P, :].bitcast(I32), x_scales.rearrange("z r c -> (z r) c").bitcast(I32))
+        nc.sync.dma_start(scale_table[FIRST_SCALE_ROW:P, :].bitcast(I32), x_scales.rearrange("z r c -> r z c").bitcast(I32))
         word_table = []
         w_raw = []
 
@@ -78,15 +77,12 @@ def tile_picked_unmerge_gelu_p_kernel(tc, x_words, x_scales, w1, res, offs, own,
             res_sb[b, lo] = shared.tile([P, hi - lo], F32, name=f"res{b}_{lo}", offset=offset)
             nc.sync.dma_start(res_sb[b, lo][:], res[b * P : (b + 1) * P, lo:hi])
 
-        def move_scales(z):
-            for q in (0, 2, 1, 3):
-                first = FIRST_SCALE_ROW + SCALE_ROWS * z + 4 * q
-                nc.sync.dma_start(planes[z][32 * q : 32 * q + 4, :].bitcast(I32), picked_scales[first : first + 4, :].bitcast(I32))
-
-        move_scales(0)
+        for q in (0, 2, 1, 3):
+            first = FIRST_SCALE_ROW + 8 * q
+            nc.sync.dma_start(planes[32 * q : 32 * q + 4, :].bitcast(I32).rearrange("p (z c) -> p z c", z=PASSES),
+                              picked_scales[first : first + 8, :].bitcast(I32))
         load_w(1, 24 * KB)
-        load_res(0, 0, 512, 28 * KB)
-        move_scales(1)
+        load_res(0, 0, 1024, 28 * KB)
 
         picked = {}
 
@@ -99,7 +95,7 @@ def tile_picked_unmerge_gelu_p_kernel(tc, x_words, x_scales, w1, res, offs, own,
             return picked[z, at][:, lo - at : hi - at]
 
         gather_words(0, 0, S, 32 * KB)
-        load_res(0, 512, U, 8 * KB)
+        load_res(0, 1024, U, 8 * KB)
 
         def res_cols(b, lo, hi):
             at = max(start for block, start in res_sb if block == b and start <= lo)
@@ -132,17 +128,21 @@ def tile_picked_unmerge_gelu_p_kernel(tc, x_words, x_scales, w1, res, offs, own,
 
         def product(b, z, lo, hi):
             if z == 0:
-                acc[b, lo] = psum.tile([P, hi - lo], F32, name=f"acc{b}_{lo}")
+                acc[b, lo] = psum.tile([P, hi - lo], F32, name=f"acc{b}_{lo}", tag="acc0_0" if (b, hi) == (1, S) else f"acc{b}_{lo}")
             codes, scales = w_q[z, b]
             nc.tensor.matmul_mx(out=acc[b, lo][:], lhsT=codes[:].bitcast(FP8X4), lhsT_scale=scales[:],
-                                rhs=picked_cols(z, lo, hi).bitcast(FP8X4), rhs_scale=planes[z][:, lo:hi],
+                                rhs=picked_cols(z, lo, hi).bitcast(FP8X4), rhs_scale=planes[:, z * S + lo : z * S + hi],
                                 start=(z == 0), stop=(z == PASSES - 1))
             if z == PASSES - 1:
                 nc.scalar.activation(y[b][:, lo:hi], acc[b, lo][:], GELU)
 
-        for b, z in ((0, 0), (1, 0), (0, 1)):
-            for lo, hi in PRODUCT_PIECES:
-                product(b, z, lo, hi)
+        for lo, hi in PRODUCT_PIECES[0]:
+            product(0, 0, lo, hi)
+        for lo, hi in PRODUCT_PIECES[1][:-1]:
+            product(1, 0, lo, hi)
+        for lo, hi in PRODUCT_PIECES[0]:
+            product(0, 1, lo, hi)
+        product(1, 0, *PRODUCT_PIECES[1][-1])
 
         total = [held.tile([P, U], F32, name=f"total{b}") for b in range(BLOCKS)]
         fetched = {}
@@ -160,7 +160,7 @@ def tile_picked_unmerge_gelu_p_kernel(tc, x_words, x_scales, w1, res, offs, own,
         def store(b, lo, hi):
             nc.sync.dma_start(out[b * P : (b + 1) * P, lo:hi], total[b][:, lo:hi])
 
-        for lo, hi in PRODUCT_PIECES:
+        for lo, hi in PRODUCT_PIECES[1]:
             product(1, 1, lo, hi)
         fetch(0, 1536, 2048)
         for lo, hi in ((0, 512), (512, 1024), (1280, 1664), (1664, 1920), (1920, 2048)):

@@ -24,7 +24,8 @@ BLOCKS = N // P
 LIST_ROWS = 16
 SCALE_ROWS = 16
 FIRST_SCALE_ROW = P - PASSES * SCALE_ROWS
-PRODUCT_PIECES = (((0, 256), (256, 512), (512, 768), (768, 896), (896, 1024)), ((0, 512), (512, 768), (768, 896), (896, 1024)))
+PRODUCT_PIECES = (((0, 256), (256, 512), (512, 768), (768, 896), (896, 1024)), ((0, 512), (512, 768), (768, 1024)))
+BANK = {(0, 0): 0, (0, 256): 1, (0, 512): 2, (0, 768): 3, (0, 896): 4, (1, 0): 5, (1, 512): 0, (1, 768): 1}
 KB = 1024
 
 
@@ -53,19 +54,21 @@ def tile_picked_unmerge_gelu_p_kernel(tc, x_words, x_scales, w1, res, offs, own,
         nc.sync.dma_start(offs_sb[:], offs)
         nc.sync.dma_start(scale_table[FIRST_SCALE_ROW:P, :].bitcast(I32), x_scales.rearrange("z r c -> r z c").bitcast(I32))
         word_table = []
-        w_raw = []
+        w_raw = {}
 
-        def load_w(z, offset):
-            raw = shared.tile([P, PACK, N], F32, name=f"w_raw{z}", offset=offset)
-            nc.sync.dma_start(raw[:], w1[z * K_PASS : (z + 1) * K_PASS, :].rearrange("(p j) c -> p j c", j=PACK))
-            w_raw.append(raw)
+        def load_w(z, blocks, offset):
+            lo, hi = blocks[0] * P, (blocks[-1] + 1) * P
+            raw = shared.tile([P, PACK, hi - lo], F32, name=f"w_raw{z}{blocks[0]}", offset=offset)
+            nc.sync.dma_start(raw[:], w1[z * K_PASS : (z + 1) * K_PASS, lo:hi].rearrange("(p j) c -> p j c", j=PACK))
+            for b in blocks:
+                w_raw[z, b] = raw[:, :, b * P - lo : (b + 1) * P - lo]
 
         for z in range(PASSES):
             table = shared.tile([P, T], I32, name=f"word_table{z}", offset=(8 + 8 * z) * KB)
             nc.sync.dma_start(table[:], x_words[z].rearrange("p c r -> p (c r)").bitcast(I32))
             word_table.append(table)
             if z == 0:
-                load_w(0, 0)
+                load_w(0, (0, 1), 0)
         nc.sync.dma_start(own_sb[:], own)
 
         picked_scales = held.tile([P, S], U8, name="picked_scales", align_bytes=64)
@@ -81,8 +84,8 @@ def tile_picked_unmerge_gelu_p_kernel(tc, x_words, x_scales, w1, res, offs, own,
             first = FIRST_SCALE_ROW + 8 * q
             nc.sync.dma_start(planes[32 * q : 32 * q + 4, :].bitcast(I32).rearrange("p (z c) -> p z c", z=PASSES),
                               picked_scales[first : first + 8, :].bitcast(I32))
-        load_w(1, 24 * KB)
-        load_res(0, 0, 1024, 28 * KB)
+        load_w(1, (0,), 26 * KB)
+        load_w(1, (1,), 28 * KB)
 
         picked = {}
 
@@ -95,7 +98,8 @@ def tile_picked_unmerge_gelu_p_kernel(tc, x_words, x_scales, w1, res, offs, own,
             return picked[z, at][:, lo - at : hi - at]
 
         gather_words(0, 0, S, 32 * KB)
-        load_res(0, 1024, U, 8 * KB)
+        load_res(0, 0, 1024, 8 * KB)
+        load_res(0, 1024, U, 12 * KB)
 
         def res_cols(b, lo, hi):
             at = max(start for block, start in res_sb if block == b and start <= lo)
@@ -104,7 +108,7 @@ def tile_picked_unmerge_gelu_p_kernel(tc, x_words, x_scales, w1, res, offs, own,
         def cast_w(z, b, copy, offset):
             grouped = shared.tile([P, P * PACK], BF16, name=f"w_bf{z}{b}", offset=offset, align_bytes=64)
             copy(grouped[:].rearrange("p (c i j) -> p c j i", i=4, j=PACK),
-                 w_raw[z][:, :, b * P : (b + 1) * P].rearrange("p j (c i) -> p c j i", i=4))
+                 w_raw[z, b].rearrange("p j (c i) -> p c j i", i=4))
             return grouped
 
         def quantize_w(z, b, grouped):
@@ -117,18 +121,18 @@ def tile_picked_unmerge_gelu_p_kernel(tc, x_words, x_scales, w1, res, offs, own,
         for b in range(BLOCKS):
             w_q[0, b] = quantize_w(0, b, cast_w(0, b, nc.scalar.copy, (40 + b) * KB))
         load_res(1, 0, U, 0)
-        gather_words(1, 0, 896, 36 * KB)
+        gather_words(1, 0, 768, 36 * KB)
         w_q[1, 0] = quantize_w(1, 0, cast_w(1, 0, nc.scalar.copy, 42 * KB))
         grouped11 = cast_w(1, 1, nc.scalar.copy, 43 * KB)
-        gather_words(1, 896, S, 24 * KB)
+        gather_words(1, 768, S, 26 * KB)
         w_q[1, 1] = quantize_w(1, 1, grouped11)
 
-        y = [held.tile([P, S], F32, name=f"y{b}") for b in range(BLOCKS)]
+        y = [shared.tile([P, S], F32, name=f"y{b}", offset=(48 + 4 * b) * KB) for b in range(BLOCKS)]
         acc = {}
 
         def product(b, z, lo, hi):
             if z == 0:
-                acc[b, lo] = psum.tile([P, hi - lo], F32, name=f"acc{b}_{lo}", tag="acc0_0" if (b, hi) == (1, S) else f"acc{b}_{lo}")
+                acc[b, lo] = psum.tile([P, hi - lo], F32, name=f"acc{b}_{lo}", tag=f"bank{BANK[b, lo]}")
             codes, scales = w_q[z, b]
             nc.tensor.matmul_mx(out=acc[b, lo][:], lhsT=codes[:].bitcast(FP8X4), lhsT_scale=scales[:],
                                 rhs=picked_cols(z, lo, hi).bitcast(FP8X4), rhs_scale=planes[:, z * S + lo : z * S + hi],
@@ -138,50 +142,37 @@ def tile_picked_unmerge_gelu_p_kernel(tc, x_words, x_scales, w1, res, offs, own,
 
         for lo, hi in PRODUCT_PIECES[0]:
             product(0, 0, lo, hi)
-        for lo, hi in PRODUCT_PIECES[1][:-1]:
-            product(1, 0, lo, hi)
+        product(1, 0, *PRODUCT_PIECES[1][0])
         for lo, hi in PRODUCT_PIECES[0]:
             product(0, 1, lo, hi)
-        product(1, 0, *PRODUCT_PIECES[1][-1])
 
-        total = [held.tile([P, U], F32, name=f"total{b}") for b in range(BLOCKS)]
         fetched = {}
 
+        def finish(b, lo, hi, looked_up, total):
+            nc.vector.tensor_tensor(total[:], looked_up, res_cols(b, lo, hi), ADD)
+            nc.sync.dma_start(out[b * P : (b + 1) * P, lo:hi], total[:])
+
         def on_vector(b, lo, hi):
-            nc.vector.tensor_tensor(total[b][:, lo:hi], y[b][:].indirect(entries(own_sb, lo, hi)), res_cols(b, lo, hi), ADD)
+            if b == 0:
+                total = held.tile([P, hi - lo], F32, name=f"total{b}_{lo}")
+            else:
+                total = shared.tile([P, hi - lo], F32, name=f"total{b}_{lo}", offset=48 * KB + 2 * lo)
+            finish(b, lo, hi, y[b][:].indirect(entries(own_sb, lo, hi)), total)
 
         def fetch(b, lo, hi):
             fetched[b, lo] = held.tile([P, hi - lo], F32, name=f"fetched{b}_{lo}")
             nc.scalar.activation(fetched[b, lo][:], y[b][:].indirect(entries(own_sb, lo, hi)), COPY)
 
         def add(b, lo, hi):
-            nc.vector.tensor_tensor(total[b][:, lo:hi], fetched[b, lo][:], res_cols(b, lo, hi), ADD)
+            finish(b, lo, hi, fetched[b, lo][:], held.tile([P, hi - lo], F32, name=f"total{b}_{lo}"))
 
-        def store(b, lo, hi):
-            nc.sync.dma_start(out[b * P : (b + 1) * P, lo:hi], total[b][:, lo:hi])
-
-        for lo, hi in PRODUCT_PIECES[1]:
-            product(1, 1, lo, hi)
-        fetch(0, 1536, 2048)
-        for lo, hi in ((0, 512), (512, 1024), (1280, 1664), (1664, 1920), (1920, 2048)):
-            fetch(1, lo, hi)
-        on_vector(0, 0, 512)
-        store(0, 0, 512)
-        on_vector(0, 512, 1024)
-        store(0, 512, 1024)
-        on_vector(0, 1024, 1536)
-        store(0, 1024, 1536)
-        add(0, 1536, 2048)
-        store(0, 1536, 2048)
-        add(1, 0, 512)
-        store(1, 0, 512)
-        add(1, 512, 1024)
-        store(1, 512, 1024)
-        on_vector(1, 1024, 1280)
-        store(1, 1024, 1280)
-        add(1, 1280, 1664)
-        store(1, 1280, 1664)
-        add(1, 1664, 1920)
-        store(1, 1664, 1920)
-        add(1, 1920, 2048)
-        store(1, 1920, 2048)
+        product(1, 1, *PRODUCT_PIECES[1][0])
+        for lo, hi in PRODUCT_PIECES[1][1:]:
+            for z in range(PASSES):
+                product(1, z, lo, hi)
+        for b, lo, hi in ((0, 1280, 1792), (0, 1792, 2048), (1, 256, 768), (1, 1024, 1408), (1, 1408, 1664), (1, 1664, 1920), (1, 1920, 2048)):
+            fetch(b, lo, hi)
+        for step, b, lo, hi in ((on_vector, 0, 0, 512), (on_vector, 0, 512, 1024), (on_vector, 0, 1024, 1280), (add, 0, 1280, 1792),
+                                (add, 0, 1792, 2048), (on_vector, 1, 0, 256), (add, 1, 256, 768), (on_vector, 1, 768, 1024),
+                                (add, 1, 1024, 1408), (add, 1, 1408, 1664), (add, 1, 1664, 1920), (add, 1, 1920, 2048)):
+            step(b, lo, hi)

@@ -24,9 +24,12 @@ BLOCKS = N // P
 LIST_ROWS = 16
 SCALE_ROWS = 16
 FIRST_SCALE_ROW = P - PASSES * SCALE_ROWS
-PRODUCT_PIECES = (((0, 256), (256, 512), (512, 768), (768, 896), (896, 1024)), ((0, 512), (512, 768), (768, 1024)))
-BANK = {(0, 0): 0, (0, 256): 1, (0, 512): 2, (0, 768): 3, (0, 896): 4, (1, 0): 5, (1, 512): 0, (1, 768): 1}
 KB = 1024
+HALF = U // 2
+SUM_PIECES = (((0, 128), (128, 384), (384, 640), (640, 896), (896, 1024)), ((0, 256), (256, 512), (512, 1024)))
+LAST_GATHER = 896
+STORES = ((0, 0, 512, 0), (0, 512, 512, 0), (1, 1024, 256, 0), (0, 1024, 0, 512), (0, 1536, 0, 512),
+          (1, 1280, 128, 256), (1, 1664, 128, 256), (1, 0, 96, 288), (1, 384, 96, 256), (1, 736, 64, 224))
 
 
 def entries(list_tile, lo, hi):
@@ -53,39 +56,33 @@ def tile_picked_unmerge_gelu_p_kernel(tc, x_words, x_scales, w1, res, offs, own,
 
         nc.sync.dma_start(offs_sb[:], offs)
         nc.sync.dma_start(scale_table[FIRST_SCALE_ROW:P, :].bitcast(I32), x_scales.rearrange("z r c -> r z c").bitcast(I32))
+
         word_table = []
         w_raw = {}
 
-        def load_w(z, blocks, offset):
-            lo, hi = blocks[0] * P, (blocks[-1] + 1) * P
-            raw = shared.tile([P, PACK, hi - lo], F32, name=f"w_raw{z}{blocks[0]}", offset=offset)
-            nc.sync.dma_start(raw[:], w1[z * K_PASS : (z + 1) * K_PASS, lo:hi].rearrange("(p j) c -> p j c", j=PACK))
-            for b in blocks:
-                w_raw[z, b] = raw[:, :, b * P - lo : (b + 1) * P - lo]
-
-        for z in range(PASSES):
-            table = shared.tile([P, T], I32, name=f"word_table{z}", offset=(8 + 8 * z) * KB)
+        def load_words(z, offset):
+            table = shared.tile([P, T], I32, name=f"word_table{z}", offset=offset)
             nc.sync.dma_start(table[:], x_words[z].rearrange("p c r -> p (c r)").bitcast(I32))
             word_table.append(table)
-            if z == 0:
-                load_w(0, (0, 1), 0)
+
+        def load_w(z, b, offset):
+            w_raw[z, b] = shared.tile([P, PACK, P], F32, name=f"w_raw{z}{b}", offset=offset)
+            nc.sync.dma_start(w_raw[z, b][:],
+                              w1[z * K_PASS : (z + 1) * K_PASS, b * P : (b + 1) * P].rearrange("(p j) c -> p j c", j=PACK))
+
+        load_words(0, 8 * KB)
+        load_w(0, 0, 0)
+        load_words(1, 40 * KB)
         nc.sync.dma_start(own_sb[:], own)
 
         picked_scales = held.tile([P, S], U8, name="picked_scales", align_bytes=64)
         nc.vector.tensor_copy(picked_scales[:], scale_table[:].indirect(offs_sb[:]))
-
-        res_sb = {}
-
-        def load_res(b, lo, hi, offset):
-            res_sb[b, lo] = shared.tile([P, hi - lo], F32, name=f"res{b}_{lo}", offset=offset)
-            nc.sync.dma_start(res_sb[b, lo][:], res[b * P : (b + 1) * P, lo:hi])
-
         for q in (0, 2, 1, 3):
             first = FIRST_SCALE_ROW + 8 * q
             nc.sync.dma_start(planes[32 * q : 32 * q + 4, :].bitcast(I32).rearrange("p (z c) -> p z c", z=PASSES),
                               picked_scales[first : first + 8, :].bitcast(I32))
-        load_w(1, (0,), 26 * KB)
-        load_w(1, (1,), 28 * KB)
+        load_w(1, 0, 26 * KB)
+        load_w(0, 1, 28 * KB)
 
         picked = {}
 
@@ -98,81 +95,81 @@ def tile_picked_unmerge_gelu_p_kernel(tc, x_words, x_scales, w1, res, offs, own,
             return picked[z, at][:, lo - at : hi - at]
 
         gather_words(0, 0, S, 32 * KB)
-        load_res(0, 0, 1024, 8 * KB)
-        load_res(0, 1024, U, 12 * KB)
+        load_w(1, 1, 8 * KB + 64)
+        res_first = shared.tile([P, HALF], F32, name="res_first", offset=10 * KB + 64)
+        nc.sync.dma_start(res_first[:], res[0:P, 0:HALF])
+        res_middle = shared.tile([P, BLOCKS, HALF], F32, name="res_middle", offset=14 * KB + 64)
+        nc.sync.dma_start(res_middle[:], res[:, HALF:U].rearrange("(b p) c -> p b c", b=BLOCKS))
+        res_last = shared.tile([P, HALF], F32, name="res_last", offset=4 * KB + 64)
+        nc.sync.dma_start(res_last[:], res[P:N, 0:HALF])
 
         def res_cols(b, lo, hi):
-            at = max(start for block, start in res_sb if block == b and start <= lo)
-            return res_sb[b, at][:, lo - at : hi - at]
+            if lo >= HALF:
+                return res_middle[:, b, lo - HALF : hi - HALF]
+            return (res_first, res_last)[b][:, lo:hi]
 
-        def cast_w(z, b, copy, offset):
-            grouped = shared.tile([P, P * PACK], BF16, name=f"w_bf{z}{b}", offset=offset, align_bytes=64)
+        def cast_w(z, b, copy):
+            grouped = held.tile([P, P * PACK], BF16, name=f"w_bf{z}{b}", align_bytes=64)
             copy(grouped[:].rearrange("p (c i j) -> p c j i", i=4, j=PACK),
-                 w_raw[z, b].rearrange("p j (c i) -> p c j i", i=4))
+                 w_raw[z, b][:].rearrange("p j (c i) -> p c j i", i=4))
             return grouped
+
+        w_q = {}
 
         def quantize_w(z, b, grouped):
             codes = held.tile([P, P], U32, name=f"w_codes{z}{b}", align_bytes=64)
             scales = held.tile([P, P], U8, name=f"w_scales{z}{b}", align_bytes=64)
             nc.vector.quantize_mx(out=codes[:].bitcast(FP8X4), scales=scales[:], in_=grouped[:])
-            return codes, scales
+            w_q[z, b] = codes, scales
 
-        w_q = {}
-        for b in range(BLOCKS):
-            w_q[0, b] = quantize_w(0, b, cast_w(0, b, nc.scalar.copy, (40 + b) * KB))
-        load_res(1, 0, U, 0)
-        gather_words(1, 0, 768, 36 * KB)
-        w_q[1, 0] = quantize_w(1, 0, cast_w(1, 0, nc.scalar.copy, 42 * KB))
-        grouped11 = cast_w(1, 1, nc.scalar.copy, 43 * KB)
-        gather_words(1, 768, S, 26 * KB)
-        w_q[1, 1] = quantize_w(1, 1, grouped11)
+        quantize_w(0, 0, cast_w(0, 0, nc.scalar.copy))
+        gather_words(1, 0, LAST_GATHER, 36 * KB)
+        quantize_w(1, 0, cast_w(1, 0, nc.scalar.copy))
+        gather_words(1, LAST_GATHER, S, 26 * KB)
+        grouped01 = cast_w(0, 1, nc.scalar.copy)
+        grouped11 = cast_w(1, 1, nc.vector.tensor_copy)
+        quantize_w(0, 1, grouped01)
+        quantize_w(1, 1, grouped11)
 
-        y = [shared.tile([P, S], F32, name=f"y{b}", offset=(48 + 4 * b) * KB) for b in range(BLOCKS)]
+        y = [held.tile([P, S], F32, name=f"y{b}") for b in range(BLOCKS)]
         acc = {}
 
         def product(b, z, lo, hi):
             if z == 0:
-                acc[b, lo] = psum.tile([P, hi - lo], F32, name=f"acc{b}_{lo}", tag=f"bank{BANK[b, lo]}")
+                acc[b, lo] = psum.tile([P, hi - lo], F32, name=f"acc{b}_{lo}")
             codes, scales = w_q[z, b]
-            nc.tensor.matmul_mx(out=acc[b, lo][:], lhsT=codes[:].bitcast(FP8X4), lhsT_scale=scales[:],
-                                rhs=picked_cols(z, lo, hi).bitcast(FP8X4), rhs_scale=planes[:, z * S + lo : z * S + hi],
-                                start=(z == 0), stop=(z == PASSES - 1))
+            cuts = [lo, hi]
+            if z == 1 and lo < LAST_GATHER < hi:
+                cuts = sorted({lo, max(lo, LAST_GATHER - P), LAST_GATHER, hi})
+            for first, last in zip(cuts, cuts[1:]):
+                nc.tensor.matmul_mx(out=acc[b, lo][:, first - lo : last - lo], lhsT=codes[:].bitcast(FP8X4), lhsT_scale=scales[:],
+                                    rhs=picked_cols(z, first, last).bitcast(FP8X4), rhs_scale=planes[:, z * S + first : z * S + last],
+                                    start=(z == 0), stop=(z == PASSES - 1 and last == hi))
             if z == PASSES - 1:
                 nc.scalar.activation(y[b][:, lo:hi], acc[b, lo][:], GELU)
 
-        for lo, hi in PRODUCT_PIECES[0]:
-            product(0, 0, lo, hi)
-        product(1, 0, *PRODUCT_PIECES[1][0])
-        for lo, hi in PRODUCT_PIECES[0]:
-            product(0, 1, lo, hi)
-
-        fetched = {}
-
-        def finish(b, lo, hi, looked_up, total):
-            nc.vector.tensor_tensor(total[:], looked_up, res_cols(b, lo, hi), ADD)
-            nc.sync.dma_start(out[b * P : (b + 1) * P, lo:hi], total[:])
-
-        def on_vector(b, lo, hi):
-            if b == 0:
-                total = held.tile([P, hi - lo], F32, name=f"total{b}_{lo}")
-            else:
-                total = shared.tile([P, hi - lo], F32, name=f"total{b}_{lo}", offset=48 * KB + 2 * lo)
-            finish(b, lo, hi, y[b][:].indirect(entries(own_sb, lo, hi)), total)
-
-        def fetch(b, lo, hi):
-            fetched[b, lo] = held.tile([P, hi - lo], F32, name=f"fetched{b}_{lo}")
-            nc.scalar.activation(fetched[b, lo][:], y[b][:].indirect(entries(own_sb, lo, hi)), COPY)
-
-        def add(b, lo, hi):
-            finish(b, lo, hi, fetched[b, lo][:], held.tile([P, hi - lo], F32, name=f"total{b}_{lo}"))
-
-        product(1, 1, *PRODUCT_PIECES[1][0])
-        for lo, hi in PRODUCT_PIECES[1][1:]:
+        for z in range(PASSES):
+            for lo, hi in SUM_PIECES[0]:
+                product(0, z, lo, hi)
+        for lo, hi in SUM_PIECES[1]:
             for z in range(PASSES):
                 product(1, z, lo, hi)
-        for b, lo, hi in ((0, 1280, 1792), (0, 1792, 2048), (1, 256, 768), (1, 1024, 1408), (1, 1408, 1664), (1, 1664, 1920), (1, 1920, 2048)):
-            fetch(b, lo, hi)
-        for step, b, lo, hi in ((on_vector, 0, 0, 512), (on_vector, 0, 512, 1024), (on_vector, 0, 1024, 1280), (add, 0, 1280, 1792),
-                                (add, 0, 1792, 2048), (on_vector, 1, 0, 256), (add, 1, 256, 768), (on_vector, 1, 768, 1024),
-                                (add, 1, 1024, 1408), (add, 1, 1408, 1664), (add, 1, 1664, 1920), (add, 1, 1920, 2048)):
-            step(b, lo, hi)
+
+        fetched = {}
+        slot = {}
+        for n, (b, lo, on_vector, on_scalar) in enumerate(STORES):
+            if on_scalar:
+                slot[n] = (48 + 2 * len(slot)) * KB
+                fetched[n] = shared.tile([P, on_scalar], F32, name=f"fetched{n}", offset=slot[n])
+                nc.scalar.activation(fetched[n][:], y[b][:].indirect(entries(own_sb, lo + on_vector, lo + on_vector + on_scalar)), COPY)
+        for n, (b, lo, on_vector, on_scalar) in enumerate(STORES):
+            mid, hi = lo + on_vector, lo + on_vector + on_scalar
+            if on_vector and on_scalar:
+                total = shared.tile([P, hi - lo], F32, name=f"total{n}", offset=slot[n - 2])
+            else:
+                total = held.tile([P, hi - lo], F32, name=f"total{n}")
+            if on_vector:
+                nc.vector.tensor_tensor(total[:, 0:on_vector], y[b][:].indirect(entries(own_sb, lo, mid)), res_cols(b, lo, mid), ADD)
+            if on_scalar:
+                nc.vector.tensor_tensor(total[:, on_vector : hi - lo], fetched[n][:], res_cols(b, mid, hi), ADD)
+            nc.sync.dma_start(out[b * P : (b + 1) * P, lo:hi], total[:])

@@ -28,8 +28,8 @@ KB = 1024
 HALF = U // 2
 SUM_PIECES = (((0, 128), (128, 384), (384, 640), (640, 896), (896, 1024)), ((0, 256), (256, 512), (512, 1024)))
 LAST_GATHER = 896
-STORES = ((0, 0, 512, 0), (0, 512, 512, 0), (1, 1024, 256, 0), (0, 1024, 0, 512), (0, 1536, 0, 512),
-          (1, 1280, 128, 256), (1, 1664, 128, 256), (1, 0, 96, 288), (1, 384, 96, 256), (1, 736, 64, 224))
+STORES = ((0, 0, 512, 0), (0, 512, 512, 0), (1, 1792, 256, 0), (0, 1024, 0, 512), (0, 1536, 0, 512),
+          (1, 1024, 128, 256), (1, 1408, 128, 256), (1, 0, 96, 288), (1, 384, 96, 256), (1, 736, 64, 224))
 
 
 def entries(list_tile, lo, hi):

@@ -20,16 +20,27 @@ P = 128
 PACK = 4
 K_PASS = P * PACK
 PASSES = K // K_PASS
-BLOCKS = N // P
+HALVES = N // P
 LIST_ROWS = 16
 SCALE_ROWS = 16
+QUADRANT = 32
+QUADRANT_ROWS = 4
 FIRST_SCALE_ROW = P - PASSES * SCALE_ROWS
+MID = U // 2
 KB = 1024
-HALF = U // 2
-SUM_PIECES = (((0, 128), (128, 384), (384, 640), (640, 896), (896, 1024)), ((0, 256), (256, 512), (512, 1024)))
-LAST_GATHER = 896
+
+EARLY_WORDS = 768
+SUM_PIECES = (((0, 256), (256, 512), (512, 768), (768, 1024)), ((0, 128), (128, 256), (256, 512), (512, 1024)))
 STORES = ((0, 0, 512, 0), (0, 512, 512, 0), (1, 1792, 256, 0), (0, 1024, 0, 512), (0, 1536, 0, 512),
           (1, 1024, 128, 256), (1, 1408, 128, 256), (1, 0, 96, 288), (1, 384, 96, 256), (1, 736, 64, 224))
+
+APART = 64
+AT_W_RAW = {(0, 0): 0, (1, 0): 26 * KB, (0, 1): 28 * KB, (1, 1): 8 * KB + APART}
+AT_WORD_TABLE = (8 * KB, 40 * KB)
+AT_SCALE_TABLE = 27 * KB
+AT_RES_FIRST, AT_RES_MIDDLE, AT_RES_LAST = 10 * KB + APART, 14 * KB + APART, 4 * KB + APART
+AT_PICKED_0, AT_PICKED_EARLY, AT_PICKED_LATE = 32 * KB, 36 * KB, AT_W_RAW[1, 0]
+AT_FETCHED, FETCHED_BYTES = 48 * KB, 2 * KB
 
 
 def entries(list_tile, lo, hi):
@@ -45,10 +56,10 @@ def tile_picked_unmerge_gelu_p_kernel(tc, x_words, x_scales, w1, res, offs, own,
 
         offs_sb = held.tile([P, S // LIST_ROWS], U16, name="offs_sb")
         own_sb = held.tile([P, U // LIST_ROWS], U16, name="own_sb")
-        scale_table = shared.tile([P, T], U8, name="scale_table", offset=27 * KB)
+        scale_table = shared.tile([P, T], U8, name="scale_table", offset=AT_SCALE_TABLE)
         nc.vector.memset(scale_table[0:FIRST_SCALE_ROW, :].bitcast(I32), 0)
-        planes = held.tile([P, PASSES * S], U8, name="planes", align_bytes=64)
-        nc.vector.memset(planes[:].bitcast(I32), 0)
+        x_scale_rows = held.tile([P, PASSES * S], U8, name="x_scale_rows", align_bytes=64)
+        nc.vector.memset(x_scale_rows[:].bitcast(I32), 0)
         warm_in = held.tile([P, 1], F32, name="warm_in")
         warm_out = held.tile([P, 1], F32, name="warm_out")
         nc.vector.memset(warm_in[:], 0.0)
@@ -60,29 +71,30 @@ def tile_picked_unmerge_gelu_p_kernel(tc, x_words, x_scales, w1, res, offs, own,
         word_table = []
         w_raw = {}
 
-        def load_words(z, offset):
-            table = shared.tile([P, T], I32, name=f"word_table{z}", offset=offset)
+        def load_words(z):
+            table = shared.tile([P, T], I32, name=f"word_table{z}", offset=AT_WORD_TABLE[z])
             nc.sync.dma_start(table[:], x_words[z].rearrange("p c r -> p (c r)").bitcast(I32))
             word_table.append(table)
 
-        def load_w(z, b, offset):
-            w_raw[z, b] = shared.tile([P, PACK, P], F32, name=f"w_raw{z}{b}", offset=offset)
-            nc.sync.dma_start(w_raw[z, b][:],
-                              w1[z * K_PASS : (z + 1) * K_PASS, b * P : (b + 1) * P].rearrange("(p j) c -> p j c", j=PACK))
+        def load_w(z, half):
+            w_raw[z, half] = shared.tile([P, PACK, P], F32, name=f"w_raw{z}{half}", offset=AT_W_RAW[z, half])
+            nc.sync.dma_start(w_raw[z, half][:],
+                              w1[z * K_PASS : (z + 1) * K_PASS, half * P : (half + 1) * P].rearrange("(p j) c -> p j c", j=PACK))
 
-        load_words(0, 8 * KB)
-        load_w(0, 0, 0)
-        load_words(1, 40 * KB)
+        load_words(0)
+        load_w(0, 0)
+        load_words(1)
         nc.sync.dma_start(own_sb[:], own)
 
         picked_scales = held.tile([P, S], U8, name="picked_scales", align_bytes=64)
         nc.vector.tensor_copy(picked_scales[:], scale_table[:].indirect(offs_sb[:]))
         for q in (0, 2, 1, 3):
-            first = FIRST_SCALE_ROW + 8 * q
-            nc.sync.dma_start(planes[32 * q : 32 * q + 4, :].bitcast(I32).rearrange("p (z c) -> p z c", z=PASSES),
-                              picked_scales[first : first + 8, :].bitcast(I32))
-        load_w(1, 0, 26 * KB)
-        load_w(0, 1, 28 * KB)
+            source = FIRST_SCALE_ROW + PASSES * QUADRANT_ROWS * q
+            nc.sync.dma_start(
+                x_scale_rows[QUADRANT * q : QUADRANT * q + QUADRANT_ROWS, :].bitcast(I32).rearrange("p (z c) -> p z c", z=PASSES),
+                picked_scales[source : source + PASSES * QUADRANT_ROWS, :].bitcast(I32))
+        load_w(1, 0)
+        load_w(0, 1)
 
         picked = {}
 
@@ -94,59 +106,60 @@ def tile_picked_unmerge_gelu_p_kernel(tc, x_words, x_scales, w1, res, offs, own,
             at = max(start for zz, start in picked if zz == z and start <= lo)
             return picked[z, at][:, lo - at : hi - at]
 
-        gather_words(0, 0, S, 32 * KB)
-        load_w(1, 1, 8 * KB + 64)
-        res_first = shared.tile([P, HALF], F32, name="res_first", offset=10 * KB + 64)
-        nc.sync.dma_start(res_first[:], res[0:P, 0:HALF])
-        res_middle = shared.tile([P, BLOCKS, HALF], F32, name="res_middle", offset=14 * KB + 64)
-        nc.sync.dma_start(res_middle[:], res[:, HALF:U].rearrange("(b p) c -> p b c", b=BLOCKS))
-        res_last = shared.tile([P, HALF], F32, name="res_last", offset=4 * KB + 64)
-        nc.sync.dma_start(res_last[:], res[P:N, 0:HALF])
+        gather_words(0, 0, S, AT_PICKED_0)
+        load_w(1, 1)
+        res_first = shared.tile([P, MID], F32, name="res_first", offset=AT_RES_FIRST)
+        nc.sync.dma_start(res_first[:], res[0:P, 0:MID])
+        res_middle = shared.tile([P, HALVES, MID], F32, name="res_middle", offset=AT_RES_MIDDLE)
+        nc.sync.dma_start(res_middle[:], res[:, MID:U].rearrange("(b p) c -> p b c", b=HALVES))
+        res_last = shared.tile([P, MID], F32, name="res_last", offset=AT_RES_LAST)
+        nc.sync.dma_start(res_last[:], res[P:N, 0:MID])
 
-        def res_cols(b, lo, hi):
-            if lo >= HALF:
-                return res_middle[:, b, lo - HALF : hi - HALF]
-            return (res_first, res_last)[b][:, lo:hi]
+        def res_cols(half, lo, hi):
+            if lo >= MID:
+                return res_middle[:, half, lo - MID : hi - MID]
+            return (res_first, res_last)[half][:, lo:hi]
 
-        def cast_w(z, b, copy):
-            grouped = held.tile([P, P * PACK], BF16, name=f"w_bf{z}{b}", align_bytes=64)
+        def round_w(z, half, copy):
+            grouped = held.tile([P, P * PACK], BF16, name=f"w_bf{z}{half}", align_bytes=64)
             copy(grouped[:].rearrange("p (c i j) -> p c j i", i=4, j=PACK),
-                 w_raw[z, b][:].rearrange("p j (c i) -> p c j i", i=4))
+                 w_raw[z, half][:].rearrange("p j (c i) -> p c j i", i=4))
             return grouped
 
         w_q = {}
 
-        def quantize_w(z, b, grouped):
-            codes = held.tile([P, P], U32, name=f"w_codes{z}{b}", align_bytes=64)
-            scales = held.tile([P, P], U8, name=f"w_scales{z}{b}", align_bytes=64)
+        def quantize_w(z, half, grouped):
+            codes = held.tile([P, P], U32, name=f"w_codes{z}{half}", align_bytes=64)
+            scales = held.tile([P, P], U8, name=f"w_scales{z}{half}", align_bytes=64)
             nc.vector.quantize_mx(out=codes[:].bitcast(FP8X4), scales=scales[:], in_=grouped[:])
-            w_q[z, b] = codes, scales
+            w_q[z, half] = codes, scales
 
-        quantize_w(0, 0, cast_w(0, 0, nc.scalar.copy))
-        gather_words(1, 0, LAST_GATHER, 36 * KB)
-        quantize_w(1, 0, cast_w(1, 0, nc.scalar.copy))
-        gather_words(1, LAST_GATHER, S, 26 * KB)
-        grouped01 = cast_w(0, 1, nc.scalar.copy)
-        grouped11 = cast_w(1, 1, nc.vector.tensor_copy)
+        quantize_w(0, 0, round_w(0, 0, nc.scalar.copy))
+        gather_words(1, 0, EARLY_WORDS, AT_PICKED_EARLY)
+        quantize_w(1, 0, round_w(1, 0, nc.scalar.copy))
+        gather_words(1, EARLY_WORDS, S, AT_PICKED_LATE)
+        grouped01 = round_w(0, 1, nc.scalar.copy)
+        grouped11 = round_w(1, 1, nc.vector.tensor_copy)
         quantize_w(0, 1, grouped01)
         quantize_w(1, 1, grouped11)
 
-        y = [held.tile([P, S], F32, name=f"y{b}") for b in range(BLOCKS)]
+        y = [held.tile([P, S], F32, name=f"y{half}") for half in range(HALVES)]
         acc = {}
 
-        def product(b, z, lo, hi):
+        def product(half, z, lo, hi):
             if z == 0:
-                acc[b, lo] = psum.tile([P, hi - lo], F32, name=f"acc{b}_{lo}")
-            codes, scales = w_q[z, b]
+                acc[half, lo] = psum.tile([P, hi - lo], F32, name=f"acc{half}_{lo}")
+            codes, scales = w_q[z, half]
             cuts = [lo, hi]
-            if z == 1 and lo < LAST_GATHER < hi:
-                cuts = sorted({lo, max(lo, LAST_GATHER - P), LAST_GATHER, hi})
+            if z == 1 and lo < EARLY_WORDS < hi:
+                cuts = [lo, EARLY_WORDS, hi]
             for first, last in zip(cuts, cuts[1:]):
-                nc.tensor.matmul_mx(out=acc[b, lo][:, first - lo : last - lo], lhsT=codes[:].bitcast(FP8X4), lhsT_scale=scales[:],
-                                    rhs=picked_cols(z, first, last).bitcast(FP8X4), rhs_scale=planes[:, z * S + first : z * S + last],
+                nc.tensor.matmul_mx(out=acc[half, lo][:, first - lo : last - lo], lhsT=codes[:].bitcast(FP8X4), lhsT_scale=scales[:],
+                                    rhs=picked_cols(z, first, last).bitcast(FP8X4),
+                                    rhs_scale=x_scale_rows[:, z * S + first : z * S + last],
                                     start=(z == 0), stop=(z == PASSES - 1 and last == hi))
             if z == PASSES - 1:
-                nc.scalar.activation(y[b][:, lo:hi], acc[b, lo][:], GELU)
+                nc.scalar.activation(y[half][:, lo:hi], acc[half, lo][:], GELU)
 
         for z in range(PASSES):
             for lo, hi in SUM_PIECES[0]:
@@ -156,20 +169,20 @@ def tile_picked_unmerge_gelu_p_kernel(tc, x_words, x_scales, w1, res, offs, own,
                 product(1, z, lo, hi)
 
         fetched = {}
-        slot = {}
-        for n, (b, lo, on_vector, on_scalar) in enumerate(STORES):
+        fetched_at = {}
+        for n, (half, lo, on_vector, on_scalar) in enumerate(STORES):
             if on_scalar:
-                slot[n] = (48 + 2 * len(slot)) * KB
-                fetched[n] = shared.tile([P, on_scalar], F32, name=f"fetched{n}", offset=slot[n])
-                nc.scalar.activation(fetched[n][:], y[b][:].indirect(entries(own_sb, lo + on_vector, lo + on_vector + on_scalar)), COPY)
-        for n, (b, lo, on_vector, on_scalar) in enumerate(STORES):
+                fetched_at[n] = AT_FETCHED + FETCHED_BYTES * len(fetched_at)
+                fetched[n] = shared.tile([P, on_scalar], F32, name=f"fetched{n}", offset=fetched_at[n])
+                nc.scalar.activation(fetched[n][:], y[half][:].indirect(entries(own_sb, lo + on_vector, lo + on_vector + on_scalar)), COPY)
+        for n, (half, lo, on_vector, on_scalar) in enumerate(STORES):
             mid, hi = lo + on_vector, lo + on_vector + on_scalar
             if on_vector and on_scalar:
-                total = shared.tile([P, hi - lo], F32, name=f"total{n}", offset=slot[n - 2])
+                total = shared.tile([P, hi - lo], F32, name=f"total{n}", offset=fetched_at[n - 2])
             else:
                 total = held.tile([P, hi - lo], F32, name=f"total{n}")
             if on_vector:
-                nc.vector.tensor_tensor(total[:, 0:on_vector], y[b][:].indirect(entries(own_sb, lo, mid)), res_cols(b, lo, mid), ADD)
+                nc.vector.tensor_tensor(total[:, 0:on_vector], y[half][:].indirect(entries(own_sb, lo, mid)), res_cols(half, lo, mid), ADD)
             if on_scalar:
-                nc.vector.tensor_tensor(total[:, on_vector : hi - lo], fetched[n][:], res_cols(b, mid, hi), ADD)
-            nc.sync.dma_start(out[b * P : (b + 1) * P, lo:hi], total[:])
+                nc.vector.tensor_tensor(total[:, on_vector : hi - lo], fetched[n][:], res_cols(half, mid, hi), ADD)
+            nc.sync.dma_start(out[half * P : (half + 1) * P, lo:hi], total[:])

@@ -34,7 +34,7 @@ SUM_PIECES = (((0, 256), (256, 512), (512, 768), (768, 1024)), ((0, 128), (128, 
 STORES = ((0, 0, 512, 0), (0, 512, 512, 0), (1, 1792, 256, 0), (0, 1024, 0, 512), (0, 1536, 0, 512),
           (1, 1024, 128, 256), (1, 1408, 128, 256), (1, 0, 96, 288), (1, 384, 96, 256), (1, 736, 64, 224))
 
-APART = 64
+APART = 256
 AT_W_RAW = {(0, 0): 0, (1, 0): 26 * KB, (0, 1): 28 * KB, (1, 1): 8 * KB + APART}
 AT_WORD_TABLE = (8 * KB, 40 * KB)
 AT_SCALE_TABLE = 27 * KB
@@ -54,11 +54,11 @@ def tile_picked_unmerge_gelu_p_kernel(tc, x_words, x_scales, w1, res, offs, own,
         shared = ctx.enter_context(tc.tile_pool(name="shared", bufs=1))
         psum = ctx.enter_context(tc.psum_pool(name="psum", bufs=1))
 
-        offs_sb = held.tile([P, S // LIST_ROWS], U16, name="offs_sb")
-        own_sb = held.tile([P, U // LIST_ROWS], U16, name="own_sb")
+        offs_sb = held.tile([P, S // LIST_ROWS], U16, name="offs_sb", align_bytes=256)
+        own_sb = held.tile([P, U // LIST_ROWS], U16, name="own_sb", align_bytes=256)
         scale_table = shared.tile([P, T], U8, name="scale_table", offset=AT_SCALE_TABLE)
         nc.vector.memset(scale_table[0:FIRST_SCALE_ROW, :].bitcast(I32), 0)
-        x_scale_rows = held.tile([P, PASSES * S], U8, name="x_scale_rows", align_bytes=64)
+        x_scale_rows = held.tile([P, PASSES * S], U8, name="x_scale_rows", align_bytes=256)
         nc.vector.memset(x_scale_rows[:].bitcast(I32), 0)
         warm_in = held.tile([P, 1], F32, name="warm_in")
         warm_out = held.tile([P, 1], F32, name="warm_out")
@@ -86,7 +86,7 @@ def tile_picked_unmerge_gelu_p_kernel(tc, x_words, x_scales, w1, res, offs, own,
         load_words(1)
         nc.sync.dma_start(own_sb[:], own)
 
-        picked_scales = held.tile([P, S], U8, name="picked_scales", align_bytes=64)
+        picked_scales = held.tile([P, S], U8, name="picked_scales", align_bytes=256)
         nc.vector.tensor_copy(picked_scales[:], scale_table[:].indirect(offs_sb[:]))
         for q in (0, 2, 1, 3):
             source = FIRST_SCALE_ROW + PASSES * QUADRANT_ROWS * q
@@ -99,7 +99,7 @@ def tile_picked_unmerge_gelu_p_kernel(tc, x_words, x_scales, w1, res, offs, own,
         picked = {}
 
         def gather_words(z, lo, hi, offset):
-            picked[z, lo] = shared.tile([P, hi - lo], U32, name=f"picked{z}_{lo}", offset=offset, align_bytes=64)
+            picked[z, lo] = shared.tile([P, hi - lo], U32, name=f"picked{z}_{lo}", offset=offset, align_bytes=256)
             nc.vector.tensor_copy(picked[z, lo][:], word_table[z][:].bitcast(U32).indirect(entries(offs_sb, lo, hi)))
 
         def picked_cols(z, lo, hi):
@@ -180,7 +180,7 @@ def tile_picked_unmerge_gelu_p_kernel(tc, x_words, x_scales, w1, res, offs, own,
             if on_vector and on_scalar:
                 total = shared.tile([P, hi - lo], F32, name=f"total{n}", offset=fetched_at[n - 2])
             else:
-                total = held.tile([P, hi - lo], F32, name=f"total{n}")
+                total = held.tile([P, hi - lo], F32, name=f"total{n}", align_bytes=256)
             if on_vector:
                 nc.vector.tensor_tensor(total[:, 0:on_vector], y[half][:].indirect(entries(own_sb, lo, mid)), res_cols(half, lo, mid), ADD)
             if on_scalar:

@@ -35,12 +35,14 @@ STORES = ((0, 0, 512, 0), (0, 512, 512, 0), (1, 1792, 256, 0), (0, 1024, 0, 512)
           (1, 1024, 128, 256), (1, 1408, 128, 256), (1, 0, 96, 288), (1, 384, 96, 256), (1, 736, 64, 224))
 
 APART = 256
-AT_W_RAW = {(0, 0): 0, (1, 0): 26 * KB, (0, 1): 28 * KB, (1, 1): 8 * KB + APART}
-AT_WORD_TABLE = (8 * KB, 40 * KB)
-AT_SCALE_TABLE = 27 * KB
-AT_RES_FIRST, AT_RES_MIDDLE, AT_RES_LAST = 10 * KB + APART, 14 * KB + APART, 4 * KB + APART
-AT_PICKED_0, AT_PICKED_EARLY, AT_PICKED_LATE = 32 * KB, 36 * KB, AT_W_RAW[1, 0]
-AT_FETCHED, FETCHED_BYTES = 48 * KB, 2 * KB
+STREAMS, FIRST, SECOND, THIRD = 0, 44 * KB, 108 * KB, 172 * KB
+AT_W_RAW = {(0, 0): STREAMS, (1, 0): SECOND, (0, 1): SECOND + 2 * KB, (1, 1): FIRST + 4 * KB + APART}
+AT_WORD_TABLE = (FIRST + 4 * KB, THIRD)
+AT_SCALE_TABLE = SECOND + KB
+AT_RES_FIRST, AT_RES_MIDDLE, AT_RES_LAST = FIRST + 6 * KB + APART, FIRST + 10 * KB + APART, FIRST + APART
+AT_PICKED_0, AT_PICKED_EARLY, AT_PICKED_LATE = STREAMS + 2 * KB, STREAMS + 6 * KB, AT_W_RAW[1, 0]
+AT_FETCHED, FETCHED_BYTES = STREAMS + 10 * KB, 2 * KB
+AT_Y = (SECOND + 8 * KB, THIRD + 8 * KB)
 
 
 def entries(list_tile, lo, hi):
@@ -143,7 +145,7 @@ def tile_picked_unmerge_gelu_p_kernel(tc, x_words, x_scales, w1, res, offs, own,
         quantize_w(0, 1, grouped01)
         quantize_w(1, 1, grouped11)
 
-        y = [held.tile([P, S], F32, name=f"y{half}") for half in range(HALVES)]
+        y = [shared.tile([P, S], F32, name=f"y{half}", offset=AT_Y[half]) for half in range(HALVES)]
         acc = {}
 
         def product(half, z, lo, hi):

@@ -26,20 +26,20 @@ SCALE_ROWS = 16
 QUADRANT = 32
 QUADRANT_ROWS = 4
 FIRST_SCALE_ROW = P - PASSES * SCALE_ROWS
-MID = U // 2
+MID = 640
 KB = 1024
 
 EARLY_WORDS = 768
-SUM_PIECES = (((0, 256), (256, 512), (512, 768), (768, 1024)), ((0, 128), (128, 256), (256, 512), (512, 1024)))
-STORES = ((0, 0, 512, 0), (0, 512, 512, 0), (1, 1792, 256, 0), (0, 1024, 0, 512), (0, 1536, 0, 512),
-          (1, 1024, 128, 256), (1, 1408, 128, 256), (1, 0, 96, 288), (1, 384, 96, 256), (1, 736, 64, 224))
+SUM_PIECES = (((0, 256), (256, 512), (512, 768), (768, 1024)), ((0, 128), (128, 256), (256, 512), (512, 768), (768, 1024)))
+STORES = ((0, 0, 640, 0), (1, 0, 640, 0), (0, 640, 0, 512), (0, 1152, 0, 512), (0, 1664, 128, 256),
+          (1, 640, 160, 352), (1, 1152, 128, 352), (1, 1632, 96, 192), (1, 1920, 0, 128))
 
 APART = 256
 STREAMS, FIRST, SECOND, THIRD = 0, 44 * KB, 108 * KB, 172 * KB
 AT_W_RAW = {(0, 0): STREAMS, (1, 0): SECOND, (0, 1): SECOND + 2 * KB, (1, 1): FIRST + 4 * KB + APART}
 AT_WORD_TABLE = (FIRST + 4 * KB, THIRD)
 AT_SCALE_TABLE = SECOND + KB
-AT_RES_FIRST, AT_RES_MIDDLE, AT_RES_LAST = FIRST + 6 * KB + APART, FIRST + 10 * KB + APART, FIRST + APART
+AT_RES_FIRST, AT_RES_REST = FIRST - KB + APART, FIRST + 8 * KB
 AT_PICKED_0, AT_PICKED_EARLY, AT_PICKED_LATE = STREAMS + 2 * KB, STREAMS + 6 * KB, AT_W_RAW[1, 0]
 AT_FETCHED, FETCHED_BYTES = STREAMS + 10 * KB, 2 * KB
 AT_Y = (SECOND + 8 * KB, THIRD + 8 * KB)
@@ -110,17 +110,15 @@ def tile_picked_unmerge_gelu_p_kernel(tc, x_words, x_scales, w1, res, offs, own,
 
         gather_words(0, 0, S, AT_PICKED_0)
         load_w(1, 1)
-        res_first = shared.tile([P, MID], F32, name="res_first", offset=AT_RES_FIRST)
-        nc.sync.dma_start(res_first[:], res[0:P, 0:MID])
-        res_middle = shared.tile([P, HALVES, MID], F32, name="res_middle", offset=AT_RES_MIDDLE)
-        nc.sync.dma_start(res_middle[:], res[:, MID:U].rearrange("(b p) c -> p b c", b=HALVES))
-        res_last = shared.tile([P, MID], F32, name="res_last", offset=AT_RES_LAST)
-        nc.sync.dma_start(res_last[:], res[P:N, 0:MID])
+        res_first = shared.tile([P, HALVES, MID], F32, name="res_first", offset=AT_RES_FIRST)
+        nc.sync.dma_start(res_first[:], res[:, 0:MID].rearrange("(b p) c -> p b c", b=HALVES))
+        res_rest = shared.tile([P, HALVES, U - MID], F32, name="res_rest", offset=AT_RES_REST)
+        nc.sync.dma_start(res_rest[:], res[:, MID:U].rearrange("(b p) c -> p b c", b=HALVES))
 
         def res_cols(half, lo, hi):
             if lo >= MID:
-                return res_middle[:, half, lo - MID : hi - MID]
-            return (res_first, res_last)[half][:, lo:hi]
+                return res_rest[:, half, lo - MID : hi - MID]
+            return res_first[:, half, lo:hi]
 
         def round_w(z, half, copy):
             grouped = held.tile([P, P * PACK], BF16, name=f"w_bf{z}{half}", align_bytes=64)
@@ -150,7 +148,7 @@ def tile_picked_unmerge_gelu_p_kernel(tc, x_words, x_scales, w1, res, offs, own,
 
         def product(half, z, lo, hi):
             if z == 0:
-                acc[half, lo] = psum.tile([P, hi - lo], F32, name=f"acc{half}_{lo}")
+                acc[half, lo] = psum.tile([P, hi - lo], F32, name=f"acc{half}_{lo}", tag=f"bank{len(acc) % 8}")
             codes, scales = w_q[z, half]
             cuts = [lo, hi]
             if z == 1 and lo < EARLY_WORDS < hi:

@@ -32,7 +32,7 @@ KB = 1024
 EARLY_WORDS = 768
 SUM_PIECES = (((0, 256), (256, 512), (512, 768), (768, 1024)), ((0, 128), (128, 256), (256, 512), (512, 768), (768, 1024)))
 STORES = ((0, 0, 640, 0), (1, 0, 640, 0), (0, 640, 0, 512), (0, 1152, 0, 512), (0, 1664, 128, 256),
-          (1, 640, 160, 352), (1, 1152, 128, 352), (1, 1632, 96, 192), (1, 1920, 0, 128))
+          (1, 640, 128, 352), (1, 1120, 96, 320), (1, 1536, 96, 224), (1, 1856, 64, 128))
 
 APART = 256
 STREAMS, FIRST, SECOND, THIRD = 0, 44 * KB, 108 * KB, 172 * KB
@@ -67,8 +67,8 @@ def tile_picked_unmerge_gelu_p_kernel(tc, x_words, x_scales, w1, res, offs, own,
         nc.vector.memset(warm_in[:], 0.0)
         nc.scalar.activation(warm_out[:], warm_in[:], GELU)
 
-        nc.sync.dma_start(offs_sb[:], offs)
         nc.sync.dma_start(scale_table[FIRST_SCALE_ROW:P, :].bitcast(I32), x_scales.rearrange("z r c -> r z c").bitcast(I32))
+        nc.sync.dma_start(offs_sb[:], offs)
 
         word_table = []
         w_raw = {}

from contextlib import ExitStack

import concourse.mybir as mybir

K, T, S, N, U = 1024, 2048, 1024, 256, 2048
FLOPS = 2 * K * N * S

F32 = mybir.dt.float32
BF16 = mybir.dt.bfloat16
I32 = mybir.dt.int32
U32 = mybir.dt.uint32
U16 = mybir.dt.uint16
U8 = mybir.dt.uint8
FP8X4 = mybir.dt.float8_e4m3fn_x4
GELU = mybir.ActivationFunctionType.Gelu_apprx_tanh
COPY = mybir.ActivationFunctionType.Copy
ADD = mybir.AluOpType.add

P = 128
PACK = 4
K_PASS = P * PACK
PASSES = K // K_PASS
HALVES = N // P
LIST_ROWS = 16
SCALE_ROWS = 16
QUADRANT = 32
QUADRANT_ROWS = 4
FIRST_SCALE_ROW = P - PASSES * SCALE_ROWS
MID = 640
KB = 1024

EARLY_WORDS = 768
SUM_PIECES = (((0, 256), (256, 512), (512, 768), (768, 1024)), ((0, 128), (128, 256), (256, 512), (512, 768), (768, 1024)))
STORES = ((0, 0, 640, 0), (1, 0, 640, 0), (0, 640, 0, 512), (0, 1152, 0, 512), (0, 1664, 128, 256),
          (1, 640, 128, 352), (1, 1120, 96, 320), (1, 1536, 96, 224), (1, 1856, 64, 128))

APART = 256
STREAMS, FIRST, SECOND, THIRD = 0, 44 * KB, 108 * KB, 172 * KB
AT_W_RAW = {(0, 0): STREAMS, (1, 0): SECOND, (0, 1): SECOND + 2 * KB, (1, 1): FIRST + 4 * KB + APART}
AT_WORD_TABLE = (FIRST + 4 * KB, THIRD)
AT_SCALE_TABLE = SECOND + KB
AT_RES_FIRST, AT_RES_REST = FIRST - KB + APART, FIRST + 8 * KB
AT_PICKED_0, AT_PICKED_EARLY, AT_PICKED_LATE = STREAMS + 2 * KB, STREAMS + 6 * KB, AT_W_RAW[1, 0]
AT_FETCHED, FETCHED_BYTES = STREAMS + 10 * KB, 2 * KB
AT_Y = (SECOND + 8 * KB, THIRD + 8 * KB)


def entries(list_tile, lo, hi):
    return list_tile[:, lo // LIST_ROWS : hi // LIST_ROWS]


def tile_picked_unmerge_gelu_p_kernel(tc, x_words, x_scales, w1, res, offs, own, out):
    nc = tc.nc
    with ExitStack() as ctx:
        held = ctx.enter_context(tc.tile_pool(name="held", bufs=1))
        shared = ctx.enter_context(tc.tile_pool(name="shared", bufs=1))
        psum = ctx.enter_context(tc.psum_pool(name="psum", bufs=1))

        offs_sb = held.tile([P, S // LIST_ROWS], U16, name="offs_sb", align_bytes=256)
        own_sb = held.tile([P, U // LIST_ROWS], U16, name="own_sb", align_bytes=256)
        scale_table = shared.tile([P, T], U8, name="scale_table", offset=AT_SCALE_TABLE)
        nc.vector.memset(scale_table[0:FIRST_SCALE_ROW, :].bitcast(I32), 0)
        x_scale_rows = held.tile([P, PASSES * S], U8, name="x_scale_rows", align_bytes=256)
        nc.vector.memset(x_scale_rows[:].bitcast(I32), 0)
        warm_in = held.tile([P, 1], F32, name="warm_in")
        warm_out = held.tile([P, 1], F32, name="warm_out")
        nc.vector.memset(warm_in[:], 0.0)
        nc.scalar.activation(warm_out[:], warm_in[:], GELU)

        nc.sync.dma_start(scale_table[FIRST_SCALE_ROW:P, :].bitcast(I32), x_scales.rearrange("z r c -> r z c").bitcast(I32))
        nc.sync.dma_start(offs_sb[:], offs)

        word_table = []
        w_raw = {}

        def load_words(z):
            table = shared.tile([P, T], I32, name=f"word_table{z}", offset=AT_WORD_TABLE[z])
            nc.sync.dma_start(table[:], x_words[z].rearrange("p c r -> p (c r)").bitcast(I32))
            word_table.append(table)

        def load_w(z, half):
            w_raw[z, half] = shared.tile([P, PACK, P], F32, name=f"w_raw{z}{half}", offset=AT_W_RAW[z, half])
            nc.sync.dma_start(w_raw[z, half][:],
                              w1[z * K_PASS : (z + 1) * K_PASS, half * P : (half + 1) * P].rearrange("(p j) c -> p j c", j=PACK))

        load_words(0)
        load_w(0, 0)
        load_words(1)
        nc.sync.dma_start(own_sb[:], own)

        picked_scales = held.tile([P, S], U8, name="picked_scales", align_bytes=256)
        nc.vector.tensor_copy(picked_scales[:], scale_table[:].indirect(offs_sb[:]))
        for q in (0, 2, 1, 3):
            source = FIRST_SCALE_ROW + PASSES * QUADRANT_ROWS * q
            nc.sync.dma_start(
                x_scale_rows[QUADRANT * q : QUADRANT * q + QUADRANT_ROWS, :].bitcast(I32).rearrange("p (z c) -> p z c", z=PASSES),
                picked_scales[source : source + PASSES * QUADRANT_ROWS, :].bitcast(I32))
        load_w(1, 0)
        load_w(0, 1)

        picked = {}

        def gather_words(z, lo, hi, offset):
            picked[z, lo] = shared.tile([P, hi - lo], U32, name=f"picked{z}_{lo}", offset=offset, align_bytes=256)
            nc.vector.tensor_copy(picked[z, lo][:], word_table[z][:].bitcast(U32).indirect(entries(offs_sb, lo, hi)))

        def picked_cols(z, lo, hi):
            at = max(start for zz, start in picked if zz == z and start <= lo)
            return picked[z, at][:, lo - at : hi - at]

        gather_words(0, 0, S, AT_PICKED_0)
        load_w(1, 1)
        res_first = shared.tile([P, HALVES, MID], F32, name="res_first", offset=AT_RES_FIRST)
        nc.sync.dma_start(res_first[:], res[:, 0:MID].rearrange("(b p) c -> p b c", b=HALVES))
        res_rest = shared.tile([P, HALVES, U - MID], F32, name="res_rest", offset=AT_RES_REST)
        nc.sync.dma_start(res_rest[:], res[:, MID:U].rearrange("(b p) c -> p b c", b=HALVES))

        def res_cols(half, lo, hi):
            if lo >= MID:
                return res_rest[:, half, lo - MID : hi - MID]
            return res_first[:, half, lo:hi]

        def round_w(z, half, copy):
            grouped = held.tile([P, P * PACK], BF16, name=f"w_bf{z}{half}", align_bytes=64)
            copy(grouped[:].rearrange("p (c i j) -> p c j i", i=4, j=PACK),
                 w_raw[z, half][:].rearrange("p j (c i) -> p c j i", i=4))
            return grouped

        w_q = {}

        def quantize_w(z, half, grouped):
            codes = held.tile([P, P], U32, name=f"w_codes{z}{half}", align_bytes=64)
            scales = held.tile([P, P], U8, name=f"w_scales{z}{half}", align_bytes=64)
            nc.vector.quantize_mx(out=codes[:].bitcast(FP8X4), scales=scales[:], in_=grouped[:])
            w_q[z, half] = codes, scales

        quantize_w(0, 0, round_w(0, 0, nc.scalar.copy))
        gather_words(1, 0, EARLY_WORDS, AT_PICKED_EARLY)
        quantize_w(1, 0, round_w(1, 0, nc.scalar.copy))
        gather_words(1, EARLY_WORDS, S, AT_PICKED_LATE)
        grouped01 = round_w(0, 1, nc.scalar.copy)
        grouped11 = round_w(1, 1, nc.vector.tensor_copy)
        quantize_w(0, 1, grouped01)
        quantize_w(1, 1, grouped11)

        y = [shared.tile([P, S], F32, name=f"y{half}", offset=AT_Y[half]) for half in range(HALVES)]
        acc = {}

        def product(half, z, lo, hi):
            if z == 0:
                acc[half, lo] = psum.tile([P, hi - lo], F32, name=f"acc{half}_{lo}", tag=f"bank{len(acc) % 8}")
            codes, scales = w_q[z, half]
            cuts = [lo, hi]
            if z == 1 and lo < EARLY_WORDS < hi:
                cuts = [lo, EARLY_WORDS, hi]
            for first, last in zip(cuts, cuts[1:]):
                nc.tensor.matmul_mx(out=acc[half, lo][:, first - lo : last - lo], lhsT=codes[:].bitcast(FP8X4), lhsT_scale=scales[:],
                                    rhs=picked_cols(z, first, last).bitcast(FP8X4),
                                    rhs_scale=x_scale_rows[:, z * S + first : z * S + last],
                                    start=(z == 0), stop=(z == PASSES - 1 and last == hi))
            if z == PASSES - 1:
                nc.scalar.activation(y[half][:, lo:hi], acc[half, lo][:], GELU)

        for z in range(PASSES):
            for lo, hi in SUM_PIECES[0]:
                product(0, z, lo, hi)
        for lo, hi in SUM_PIECES[1]:
            for z in range(PASSES):
                product(1, z, lo, hi)

        fetched = {}
        fetched_at = {}
        for n, (half, lo, on_vector, on_scalar) in enumerate(STORES):
            if on_scalar:
                fetched_at[n] = AT_FETCHED + FETCHED_BYTES * len(fetched_at)
                fetched[n] = shared.tile([P, on_scalar], F32, name=f"fetched{n}", offset=fetched_at[n])
                nc.scalar.activation(fetched[n][:], y[half][:].indirect(entries(own_sb, lo + on_vector, lo + on_vector + on_scalar)), COPY)
        for n, (half, lo, on_vector, on_scalar) in enumerate(STORES):
            mid, hi = lo + on_vector, lo + on_vector + on_scalar
            if on_vector and on_scalar:
                total = shared.tile([P, hi - lo], F32, name=f"total{n}", offset=fetched_at[n - 2])
            else:
                total = held.tile([P, hi - lo], F32, name=f"total{n}", align_bytes=256)
            if on_vector:
                nc.vector.tensor_tensor(total[:, 0:on_vector], y[half][:].indirect(entries(own_sb, lo, mid)), res_cols(half, lo, mid), ADD)
            if on_scalar:
                nc.vector.tensor_tensor(total[:, on_vector : hi - lo], fetched[n][:], res_cols(half, mid, hi), ADD)
            nc.sync.dma_start(out[half * P : (half + 1) * P, lo:hi], total[:])
